import numpy as np
import ml_dtypes


def mxq(x, axis, fmt="e4m3"):
    dtype, down = {"e4m3": (ml_dtypes.float8_e4m3fn, 7), "e5m2": (ml_dtypes.float8_e5m2, 14)}[fmt]
    v = np.moveaxis(np.asarray(x, np.float32).astype(ml_dtypes.bfloat16).astype(np.float64), axis, -1)
    blocks = v.reshape(v.shape[:-1] + (-1, 32))
    amax = np.abs(blocks).max(-1, keepdims=True)
    byte = np.maximum(np.where(amax > 0, np.frexp(amax)[1] - 1 + 127, 0) - down, 1)
    scale = np.exp2(byte - 127.0)
    codes = (blocks / scale).astype(np.float32).astype(dtype).astype(np.float64)
    return np.moveaxis((codes * scale).reshape(v.shape), -1, axis)


WIDE = False


def mx_kscale(k):
    if not WIDE:
        return np.ones(k)
    levels = np.array([10, -10, 5, -5, 0])
    if k % 512:
        return np.exp2(np.random.permutation(np.resize(levels, k // 32))).repeat(32)
    a = np.empty((k // 512, 16))
    for p in range(k // 512):
        a[p, :8] = np.random.permutation(np.resize(levels, 8))
        for g in range(8):
            far = levels[np.abs(levels - a[p, g]) >= 10]
            a[p, g + 8] = far[np.random.randint(len(far))]
    return np.exp2(a.ravel()).repeat(32)


def f64(x):
    return np.asarray(x).astype(np.float64)


def striped(idx):
    return np.tile(idx.reshape(-1, 16).T, (8, 1)).astype(np.uint16)


def unstriped(offs):
    return offs[:16].T.reshape(-1).astype(np.int64)


def pack_weight(w):
    k, n = w.shape
    w = f64(np.asarray(w, np.float32).astype(ml_dtypes.bfloat16)).reshape(k // 32, 32, n)
    amax = np.abs(w).max(1)
    byte = np.clip(np.where(amax > 0, np.frexp(amax)[1] - 1 + 127 - 7, 1), 1, 254)
    scaled = (w * np.exp2(127.0 - byte)[:, None, :]).reshape(k, n).astype(np.float32)
    words = np.ascontiguousarray(scaled.reshape(k // 512, 128, 4, n).transpose(0, 1, 3, 2)).astype(ml_dtypes.float8_e4m3fn).view(np.uint8)
    return words, np.ascontiguousarray(byte.astype(np.uint8).reshape(k // 512, 16, n))


def unpack_weight(words, scales):
    g, p, n, _ = words.shape
    vals = np.ascontiguousarray(words).view(ml_dtypes.float8_e4m3fn).astype(np.float64) * np.repeat(np.exp2(scales.astype(np.float64) - 127.0), 8, axis=1)[..., None]
    return vals.transpose(0, 1, 3, 2).reshape(g * 512, n)


K, T, S, N, U = 1024, 1024, 512, 256, 1024


def setup_inputs():
    n = np.random.standard_normal
    s = mx_kscale(K)[:, None]
    packed_w1 = pack_weight(n((K, N)) / np.sqrt(K) / s)
    return {
        "xT": (n((K, T)) * s).astype(np.float32),
        "mem": n((N, U)).astype(np.float32),
        "w1_words": packed_w1[0],
        "w1_scales": packed_w1[1],
        "offs": striped(np.random.permutation(T)[:S]),
        "slot": striped(np.random.permutation(U)[:S]),
    }


def reference(xT, mem, w1_words, w1_scales, offs, slot):
    xq = mxq(f64(xT)[:, unstriped(offs)], 0, "e4m3")
    y = unpack_weight(w1_words, w1_scales).T @ xq
    out = f64(mem).copy()
    out[:, unstriped(slot)] = f64(mem)[:, unstriped(slot)] + y
    return out

@@ -1,0 +1,120 @@
+from contextlib import ExitStack
+
+import concourse.mybir as mybir
+
+K, T, S, N, U = 1024, 1024, 512, 256, 1024
+FLOPS = 2 * K * S * N
+
+F32 = mybir.dt.float32
+BF16 = mybir.dt.bfloat16
+I32 = mybir.dt.int32
+U32 = mybir.dt.uint32
+U16 = mybir.dt.uint16
+U8 = mybir.dt.uint8
+FP8X4 = mybir.dt.float8_e4m3fn_x4
+ADD = mybir.AluOpType.add
+
+P = 128
+PACK = 4
+PASSES = K // (P * PACK)
+BLOCKS = N // P
+HALVES = 2
+H = S // HALVES
+HC = H // 16
+RUN = 4
+
+
+def tile_picked_idxput_add_e_kernel(tc, xT, mem, w1_words, w1_scales, offs, slot, out):
+    nc = tc.nc
+    with ExitStack() as ctx:
+        keep = ctx.enter_context(tc.tile_pool(name="keep", bufs=1))
+        psum = ctx.enter_context(tc.psum_pool(name="psum", bufs=1))
+
+        offs_sb = keep.tile([P, S // 16], U16, name="offs_sb")
+        slot_sb = keep.tile([P, S // 16], U16, name="slot_sb")
+        w_codes = keep.tile([P, PASSES, N], U32, name="w_codes", align_bytes=64)
+        w_scales = keep.tile([P, PASSES, N], U8, name="w_scales", align_bytes=64)
+        nc.vector.memset(w_scales[:].bitcast(I32), 0)
+
+        x_rows = xT.rearrange("(z p t) c -> z t p c", z=PASSES, t=PACK)
+        planes = [[keep.tile([P, T], F32, name=f"plane{z}_{t}") for t in range(PACK)] for z in range(PASSES)]
+        store = [keep.tile([P, U], F32, name=f"store{b}") for b in range(BLOCKS)]
+
+        nc.sync.dma_start(planes[0][0][:], x_rows[0, 0])
+        nc.sync.dma_start(offs_sb[:], offs)
+        for z in range(PASSES):
+            for t in range(PACK):
+                if (z, t) != (0, 0):
+                    nc.sync.dma_start(planes[z][t][:], x_rows[z, t])
+        nc.sync.dma_start(slot_sb[:], slot)
+        nc.sync.dma_start(w_codes[:].bitcast(I32), w1_words.rearrange("z p n t -> p z (n t)").bitcast(I32))
+        for b in range(BLOCKS):
+            nc.sync.dma_start(store[b][:], mem[b * P:(b + 1) * P, :])
+        for q in range(4):
+            nc.scalar.dma_start(
+                w_scales[32 * q:32 * q + 4].bitcast(I32),
+                w1_scales[:, 4 * q:4 * q + 4, :].rearrange("z r n -> r z n").bitcast(I32),
+            )
+
+        def weave(dst, src):
+            nc.scalar.copy(
+                dst.rearrange("p (c i) t -> p c t i", i=RUN),
+                src.rearrange("p t (c i) -> p c t i", i=RUN),
+            )
+
+        def quantise(codes, scales, woven):
+            nc.vector.quantize_mx(out=codes.bitcast(FP8X4), scales=scales, in_=woven.rearrange("p c t -> p (c t)"))
+
+        picked0 = keep.tile([P, PACK, S], BF16, name="picked0")
+        for t in range(PACK):
+            nc.vector.tensor_copy(picked0[:, t, :], planes[0][t][:].indirect(offs_sb[:]))
+        woven0 = keep.tile([P, S, PACK], BF16, name="woven0", align_bytes=64)
+        weave(woven0[:], picked0[:])
+        codes0 = keep.tile([P, S], U32, name="codes0", align_bytes=64)
+        scales0 = keep.tile([P, S], U8, name="scales0", align_bytes=64)
+
+        picked1 = keep.tile([P, PACK, S], BF16, name="picked1")
+        for t in range(PACK - 1):
+            nc.vector.tensor_copy(picked1[:, t, :], planes[1][t][:].indirect(offs_sb[:]))
+            if t == 1:
+                quantise(codes0[:], scales0[:], woven0[:])
+        woven1 = [keep.tile([P, H, PACK], BF16, name=f"woven1_{h}", align_bytes=64) for h in range(HALVES)]
+        codes1 = [keep.tile([P, H], U32, name=f"codes1_{h}", align_bytes=64) for h in range(HALVES)]
+        scales1 = [keep.tile([P, H], U8, name=f"scales1_{h}", align_bytes=64) for h in range(HALVES)]
+        for h in range(HALVES):
+            nc.vector.tensor_copy(
+                picked1[:, PACK - 1, h * H:(h + 1) * H], planes[1][PACK - 1][:].indirect(offs_sb[:, h * HC:(h + 1) * HC])
+            )
+            weave(woven1[h][:], picked1[:, :, h * H:(h + 1) * H])
+
+        acc = [[psum.tile([P, H], F32, name=f"acc{h}_{b}") for b in range(BLOCKS)] for h in range(HALVES)]
+        for h in range(HALVES):
+            cols = slice(h * H, (h + 1) * H)
+            for b in range(BLOCKS):
+                rows = slice(b * P, (b + 1) * P)
+                nc.tensor.matmul_mx(
+                    out=acc[h][b][:], lhsT=w_codes[:, 0, rows].bitcast(FP8X4), lhsT_scale=w_scales[:, 0, rows],
+                    rhs=codes0[:, cols].bitcast(FP8X4), rhs_scale=scales0[:, cols], start=True, stop=False,
+                )
+
+        old = [keep.tile([P, S], F32, name=f"old{b}") for b in range(BLOCKS)]
+        y = [[keep.tile([P, H], F32, name=f"y{h}_{b}") for b in range(BLOCKS)] for h in range(HALVES)]
+        for h in range(HALVES):
+            nc.vector.tensor_copy(old[h][:], store[h][:].indirect(slot_sb[:]))
+            quantise(codes1[h][:], scales1[h][:], woven1[h][:])
+            for b in range(BLOCKS):
+                rows = slice(b * P, (b + 1) * P)
+                nc.tensor.matmul_mx(
+                    out=acc[h][b][:], lhsT=w_codes[:, 1, rows].bitcast(FP8X4), lhsT_scale=w_scales[:, 1, rows],
+                    rhs=codes1[h][:].bitcast(FP8X4), rhs_scale=scales1[h][:], start=False, stop=True,
+                )
+                nc.scalar.copy(y[h][b][:], acc[h][b][:])
+
+        for h in range(HALVES):
+            for b in range(BLOCKS):
+                nc.vector.tensor_tensor(
+                    store[b][:].indirect(slot_sb[:, h * HC:(h + 1) * HC]),
+                    y[h][b][:], old[b][:, h * H:(h + 1) * H], ADD,
+                )
+        for b in range(BLOCKS):
+            nc.sync.dma_start(out[b * P:(b + 1) * P, :], store[b][:])

@@ -22,6 +22,8 @@ HALVES = 2
 H = S // HALVES
 HC = H // 16
 RUN = 4
+BY_SCALAR = (1, 2)
+COPY = mybir.ActivationFunctionType.Copy
 
 
 def tile_picked_idxput_add_e_kernel(tc, xT, mem, w1_words, w1_scales, offs, slot, out):
@@ -34,80 +36,88 @@ def tile_picked_idxput_add_e_kernel(tc, xT, mem, w1_words, w1_scales, offs, slot
         slot_sb = keep.tile([P, S // 16], U16, name="slot_sb")
         w_codes = keep.tile([P, PASSES, N], U32, name="w_codes", align_bytes=64)
         w_scales = keep.tile([P, PASSES, N], U8, name="w_scales", align_bytes=64)
-        nc.vector.memset(w_scales[:].bitcast(I32), 0)
+        nc.gpsimd.memset(w_scales[:].bitcast(I32), 0)
 
         x_rows = xT.rearrange("(z p t) c -> z t p c", z=PASSES, t=PACK)
-        planes = [[keep.tile([P, T], F32, name=f"plane{z}_{t}") for t in range(PACK)] for z in range(PASSES)]
+        w_words = w1_words.rearrange("z p n t -> p z (n t)").bitcast(I32)
+        order = [(z, t) for z in range(PASSES) for t in range(PACK)]
+        planes = {(z, t): keep.tile([P, T], F32, name=f"plane{z}_{t}", align_bytes=64) for z, t in order}
         store = [keep.tile([P, U], F32, name=f"store{b}") for b in range(BLOCKS)]
 
-        nc.sync.dma_start(planes[0][0][:], x_rows[0, 0])
-        nc.sync.dma_start(offs_sb[:], offs)
-        for z in range(PASSES):
-            for t in range(PACK):
-                if (z, t) != (0, 0):
-                    nc.sync.dma_start(planes[z][t][:], x_rows[z, t])
-        nc.sync.dma_start(slot_sb[:], slot)
-        nc.sync.dma_start(w_codes[:].bitcast(I32), w1_words.rearrange("z p n t -> p z (n t)").bitcast(I32))
+        for z, t in order:
+            if (z, t) == order[-1]:
+                nc.sync.dma_start(slot_sb[:], slot)
+            if (z, t) == BY_SCALAR:
+                for c in range(0, T, T // 2):
+                    nc.sync.dma_start(planes[z, t][:, c:c + T // 2], x_rows[z, t][:, c:c + T // 2])
+            else:
+                nc.sync.dma_start(planes[z, t][:], x_rows[z, t])
+            if (z, t) == order[0]:
+                nc.sync.dma_start(offs_sb[:], offs)
         for b in range(BLOCKS):
             nc.sync.dma_start(store[b][:], mem[b * P:(b + 1) * P, :])
+        nc.sync.dma_start(w_codes[:].bitcast(I32), w_words)
         for q in range(4):
-            nc.scalar.dma_start(
+            nc.gpsimd.dma_start(
                 w_scales[32 * q:32 * q + 4].bitcast(I32),
                 w1_scales[:, 4 * q:4 * q + 4, :].rearrange("z r n -> r z n").bitcast(I32),
             )
 
-        def weave(dst, src):
+        picked = [keep.tile([P, PACK, S], BF16, name=f"picked{z}") for z in range(PASSES)]
+        woven0 = keep.tile([P, S, PACK], BF16, name="woven0", align_bytes=64)
+        woven1 = [keep.tile([P, H, PACK], BF16, name=f"woven1_{h}", align_bytes=64) for h in range(HALVES)]
+
+        def weave(dst, z, h):
             nc.scalar.copy(
                 dst.rearrange("p (c i) t -> p c t i", i=RUN),
-                src.rearrange("p t (c i) -> p c t i", i=RUN),
+                picked[z][:, :, h * H:(h + 1) * H].rearrange("p t (c i) -> p c t i", i=RUN),
             )
 
         def quantise(codes, scales, woven):
             nc.vector.quantize_mx(out=codes.bitcast(FP8X4), scales=scales, in_=woven.rearrange("p c t -> p (c t)"))
 
-        picked0 = keep.tile([P, PACK, S], BF16, name="picked0")
-        for t in range(PACK):
-            nc.vector.tensor_copy(picked0[:, t, :], planes[0][t][:].indirect(offs_sb[:]))
-        woven0 = keep.tile([P, S, PACK], BF16, name="woven0", align_bytes=64)
-        weave(woven0[:], picked0[:])
-        codes0 = keep.tile([P, S], U32, name="codes0", align_bytes=64)
-        scales0 = keep.tile([P, S], U8, name="scales0", align_bytes=64)
+        def gather_last_plane(z, woven_halves):
+            for h in range(HALVES):
+                nc.vector.tensor_copy(
+                    picked[z][:, PACK - 1, h * H:(h + 1) * H],
+                    planes[z, PACK - 1][:].indirect(offs_sb[:, h * HC:(h + 1) * HC]),
+                )
+                weave(woven_halves[h], z, h)
 
-        picked1 = keep.tile([P, PACK, S], BF16, name="picked1")
         for t in range(PACK - 1):
-            nc.vector.tensor_copy(picked1[:, t, :], planes[1][t][:].indirect(offs_sb[:]))
-            if t == 1:
-                quantise(codes0[:], scales0[:], woven0[:])
-        woven1 = [keep.tile([P, H, PACK], BF16, name=f"woven1_{h}", align_bytes=64) for h in range(HALVES)]
-        codes1 = [keep.tile([P, H], U32, name=f"codes1_{h}", align_bytes=64) for h in range(HALVES)]
-        scales1 = [keep.tile([P, H], U8, name=f"scales1_{h}", align_bytes=64) for h in range(HALVES)]
-        for h in range(HALVES):
-            nc.vector.tensor_copy(
-                picked1[:, PACK - 1, h * H:(h + 1) * H], planes[1][PACK - 1][:].indirect(offs_sb[:, h * HC:(h + 1) * HC])
-            )
-            weave(woven1[h][:], picked1[:, :, h * H:(h + 1) * H])
+            nc.vector.tensor_copy(picked[0][:, t, :], planes[0, t][:].indirect(offs_sb[:]))
+        gather_last_plane(0, [woven0[:, h * H:(h + 1) * H, :] for h in range(HALVES)])
+
+        for t in range(PACK - 2):
+            nc.vector.tensor_copy(picked[1][:, t, :], planes[1, t][:].indirect(offs_sb[:]))
+        codes0 = keep.tile([P, S], U32, name="plane1_1", align_bytes=64)
+        scales0 = keep.tile([P, S], U8, name="scales0", align_bytes=64)
+        quantise(codes0[:], scales0[:], woven0[:])
+
+        rounded = keep.tile([P, T], BF16, name="rounded")
+        for c in range(0, T, T // 2):
+            nc.scalar.copy(rounded[:, c:c + T // 2], planes[BY_SCALAR][:, c:c + T // 2])
+        nc.scalar.activation(picked[1][:, PACK - 2, :], rounded[:].indirect(offs_sb[:]), COPY)
+        gather_last_plane(1, [woven1[h][:] for h in range(HALVES)])
 
         acc = [[psum.tile([P, H], F32, name=f"acc{h}_{b}") for b in range(BLOCKS)] for h in range(HALVES)]
-        for h in range(HALVES):
-            cols = slice(h * H, (h + 1) * H)
-            for b in range(BLOCKS):
-                rows = slice(b * P, (b + 1) * P)
-                nc.tensor.matmul_mx(
-                    out=acc[h][b][:], lhsT=w_codes[:, 0, rows].bitcast(FP8X4), lhsT_scale=w_scales[:, 0, rows],
-                    rhs=codes0[:, cols].bitcast(FP8X4), rhs_scale=scales0[:, cols], start=True, stop=False,
-                )
+
+        def multiply(h, b, z, codes, scales):
+            nc.tensor.matmul_mx(
+                out=acc[h][b][:], lhsT=w_codes[:, z, b * P:(b + 1) * P].bitcast(FP8X4), lhsT_scale=w_scales[:, z, b * P:(b + 1) * P],
+                rhs=codes.bitcast(FP8X4), rhs_scale=scales, start=(z == 0), stop=(z == PASSES - 1),
+            )
 
         old = [keep.tile([P, S], F32, name=f"old{b}") for b in range(BLOCKS)]
         y = [[keep.tile([P, H], F32, name=f"y{h}_{b}") for b in range(BLOCKS)] for h in range(HALVES)]
         for h in range(HALVES):
             nc.vector.tensor_copy(old[h][:], store[h][:].indirect(slot_sb[:]))
-            quantise(codes1[h][:], scales1[h][:], woven1[h][:])
+            codes1 = keep.tile([P, H], U32, name=f"codes1_{h}", align_bytes=64)
+            scales1 = keep.tile([P, H], U8, name=f"scales1_{h}", align_bytes=64)
+            quantise(codes1[:], scales1[:], woven1[h][:])
             for b in range(BLOCKS):
-                rows = slice(b * P, (b + 1) * P)
-                nc.tensor.matmul_mx(
-                    out=acc[h][b][:], lhsT=w_codes[:, 1, rows].bitcast(FP8X4), lhsT_scale=w_scales[:, 1, rows],
-                    rhs=codes1[h][:].bitcast(FP8X4), rhs_scale=scales1[h][:], start=False, stop=True,
-                )
+                multiply(h, b, 0, codes0[:, h * H:(h + 1) * H], scales0[:, h * H:(h + 1) * H])
+                multiply(h, b, 1, codes1[:], scales1[:])
                 nc.scalar.copy(y[h][b][:], acc[h][b][:])
 
         for h in range(HALVES):

@@ -13,27 +13,39 @@ U16 = mybir.dt.uint16
 U8 = mybir.dt.uint8
 FP8X4 = mybir.dt.float8_e4m3fn_x4
 ADD = mybir.AluOpType.add
+COPY = mybir.ActivationFunctionType.Copy
 
 P = 128
 PACK = 4
 PASSES = K // (P * PACK)
 BLOCKS = N // P
+QUADRANT = 32
+SCALE_ROWS = 4
+ENTRIES_PER_COLUMN = 16
 HALVES = 2
 H = S // HALVES
-HC = H // 16
 RUN = 4
-BY_SCALAR = (1, 2)
-COPY = mybir.ActivationFunctionType.Copy
+BY_SCALAR = (PASSES - 1, PACK - 2)
 
 
 def tile_picked_idxput_add_e_kernel(tc, xT, mem, w1_words, w1_scales, offs, slot, out):
     nc = tc.nc
+
+    def entries(h):
+        return slice(h * H, (h + 1) * H)
+
+    def list_columns(h):
+        return slice(h * H // ENTRIES_PER_COLUMN, (h + 1) * H // ENTRIES_PER_COLUMN)
+
+    def rows(b):
+        return slice(b * P, (b + 1) * P)
+
     with ExitStack() as ctx:
         keep = ctx.enter_context(tc.tile_pool(name="keep", bufs=1))
         psum = ctx.enter_context(tc.psum_pool(name="psum", bufs=1))
 
-        offs_sb = keep.tile([P, S // 16], U16, name="offs_sb")
-        slot_sb = keep.tile([P, S // 16], U16, name="slot_sb")
+        offs_sb = keep.tile([P, S // ENTRIES_PER_COLUMN], U16, name="offs_sb")
+        slot_sb = keep.tile([P, S // ENTRIES_PER_COLUMN], U16, name="slot_sb")
         w_codes = keep.tile([P, PASSES, N], U32, name="w_codes", align_bytes=64)
         w_scales = keep.tile([P, PASSES, N], U8, name="w_scales", align_bytes=64)
         nc.gpsimd.memset(w_scales[:].bitcast(I32), 0)
@@ -43,69 +55,77 @@ def tile_picked_idxput_add_e_kernel(tc, xT, mem, w1_words, w1_scales, offs, slot
         order = [(z, t) for z in range(PASSES) for t in range(PACK)]
         planes = {(z, t): keep.tile([P, T], F32, name=f"plane{z}_{t}", align_bytes=64) for z, t in order}
         store = [keep.tile([P, U], F32, name=f"store{b}") for b in range(BLOCKS)]
+        column_halves = [slice(c, c + T // 2) for c in range(0, T, T // 2)]
 
         for z, t in order:
             if (z, t) == order[-1]:
                 nc.sync.dma_start(slot_sb[:], slot)
             if (z, t) == BY_SCALAR:
-                for c in range(0, T, T // 2):
-                    nc.sync.dma_start(planes[z, t][:, c:c + T // 2], x_rows[z, t][:, c:c + T // 2])
+                for columns in column_halves:
+                    nc.sync.dma_start(planes[z, t][:, columns], x_rows[z, t][:, columns])
             else:
                 nc.sync.dma_start(planes[z, t][:], x_rows[z, t])
             if (z, t) == order[0]:
                 nc.sync.dma_start(offs_sb[:], offs)
         for b in range(BLOCKS):
-            nc.sync.dma_start(store[b][:], mem[b * P:(b + 1) * P, :])
+            nc.sync.dma_start(store[b][:], mem[rows(b), :])
         nc.sync.dma_start(w_codes[:].bitcast(I32), w_words)
-        for q in range(4):
+        for q in range(P // QUADRANT):
             nc.gpsimd.dma_start(
-                w_scales[32 * q:32 * q + 4].bitcast(I32),
-                w1_scales[:, 4 * q:4 * q + 4, :].rearrange("z r n -> r z n").bitcast(I32),
+                w_scales[QUADRANT * q:QUADRANT * q + SCALE_ROWS].bitcast(I32),
+                w1_scales[:, SCALE_ROWS * q:SCALE_ROWS * (q + 1), :].rearrange("z r n -> r z n").bitcast(I32),
             )
 
         picked = [keep.tile([P, PACK, S], BF16, name=f"picked{z}") for z in range(PASSES)]
         woven0 = keep.tile([P, S, PACK], BF16, name="woven0", align_bytes=64)
         woven1 = [keep.tile([P, H, PACK], BF16, name=f"woven1_{h}", align_bytes=64) for h in range(HALVES)]
 
-        def weave(dst, z, h):
-            nc.scalar.copy(
-                dst.rearrange("p (c i) t -> p c t i", i=RUN),
-                picked[z][:, :, h * H:(h + 1) * H].rearrange("p t (c i) -> p c t i", i=RUN),
-            )
+        def gather_plane(z, t):
+            nc.vector.tensor_copy(picked[z][:, t, :], planes[z, t][:].indirect(offs_sb[:]))
+
+        def gather_last_plane_and_weave(z, woven_halves):
+            for h in range(HALVES):
+                nc.vector.tensor_copy(
+                    picked[z][:, PACK - 1, entries(h)], planes[z, PACK - 1][:].indirect(offs_sb[:, list_columns(h)])
+                )
+                nc.scalar.copy(
+                    woven_halves[h].rearrange("p (c i) t -> p c t i", i=RUN),
+                    picked[z][:, :, entries(h)].rearrange("p t (c i) -> p c t i", i=RUN),
+                )
 
         def quantise(codes, scales, woven):
             nc.vector.quantize_mx(out=codes.bitcast(FP8X4), scales=scales, in_=woven.rearrange("p c t -> p (c t)"))
 
-        def gather_last_plane(z, woven_halves):
-            for h in range(HALVES):
-                nc.vector.tensor_copy(
-                    picked[z][:, PACK - 1, h * H:(h + 1) * H],
-                    planes[z, PACK - 1][:].indirect(offs_sb[:, h * HC:(h + 1) * HC]),
-                )
-                weave(woven_halves[h], z, h)
-
         for t in range(PACK - 1):
-            nc.vector.tensor_copy(picked[0][:, t, :], planes[0, t][:].indirect(offs_sb[:]))
-        gather_last_plane(0, [woven0[:, h * H:(h + 1) * H, :] for h in range(HALVES)])
+            gather_plane(0, t)
+        gather_last_plane_and_weave(0, [woven0[:, entries(h), :] for h in range(HALVES)])
 
         for t in range(PACK - 2):
-            nc.vector.tensor_copy(picked[1][:, t, :], planes[1, t][:].indirect(offs_sb[:]))
+            gather_plane(1, t)
         codes0 = keep.tile([P, S], U32, name="plane1_1", align_bytes=64)
         scales0 = keep.tile([P, S], U8, name="scales0", align_bytes=64)
         quantise(codes0[:], scales0[:], woven0[:])
 
         rounded = keep.tile([P, T], BF16, name="rounded")
-        for c in range(0, T, T // 2):
-            nc.scalar.copy(rounded[:, c:c + T // 2], planes[BY_SCALAR][:, c:c + T // 2])
-        nc.scalar.activation(picked[1][:, PACK - 2, :], rounded[:].indirect(offs_sb[:]), COPY)
-        gather_last_plane(1, [woven1[h][:] for h in range(HALVES)])
+        for columns in column_halves:
+            nc.scalar.copy(rounded[:, columns], planes[BY_SCALAR][:, columns])
+        for h in range(HALVES):
+            nc.scalar.activation(
+                picked[1][:, PACK - 2, entries(h)], rounded[:].indirect(offs_sb[:, list_columns(h)]), COPY
+            )
+        gather_last_plane_and_weave(1, [woven1[h][:] for h in range(HALVES)])
 
         acc = [[psum.tile([P, H], F32, name=f"acc{h}_{b}") for b in range(BLOCKS)] for h in range(HALVES)]
 
         def multiply(h, b, z, codes, scales):
             nc.tensor.matmul_mx(
-                out=acc[h][b][:], lhsT=w_codes[:, z, b * P:(b + 1) * P].bitcast(FP8X4), lhsT_scale=w_scales[:, z, b * P:(b + 1) * P],
-                rhs=codes.bitcast(FP8X4), rhs_scale=scales, start=(z == 0), stop=(z == PASSES - 1),
+                out=acc[h][b][:],
+                lhsT=w_codes[:, z, rows(b)].bitcast(FP8X4),
+                lhsT_scale=w_scales[:, z, rows(b)],
+                rhs=codes.bitcast(FP8X4),
+                rhs_scale=scales,
+                start=(z == 0),
+                stop=(z == PASSES - 1),
             )
 
         old = [keep.tile([P, S], F32, name=f"old{b}") for b in range(BLOCKS)]
@@ -116,15 +136,14 @@ def tile_picked_idxput_add_e_kernel(tc, xT, mem, w1_words, w1_scales, offs, slot
             scales1 = keep.tile([P, H], U8, name=f"scales1_{h}", align_bytes=64)
             quantise(codes1[:], scales1[:], woven1[h][:])
             for b in range(BLOCKS):
-                multiply(h, b, 0, codes0[:, h * H:(h + 1) * H], scales0[:, h * H:(h + 1) * H])
+                multiply(h, b, 0, codes0[:, entries(h)], scales0[:, entries(h)])
                 multiply(h, b, 1, codes1[:], scales1[:])
                 nc.scalar.copy(y[h][b][:], acc[h][b][:])
 
         for h in range(HALVES):
             for b in range(BLOCKS):
                 nc.vector.tensor_tensor(
-                    store[b][:].indirect(slot_sb[:, h * HC:(h + 1) * HC]),
-                    y[h][b][:], old[b][:, h * H:(h + 1) * H], ADD,
+                    store[b][:].indirect(slot_sb[:, list_columns(h)]), y[h][b][:], old[b][:, entries(h)], ADD
                 )
         for b in range(BLOCKS):
-            nc.sync.dma_start(out[b * P:(b + 1) * P, :], store[b][:])
+            nc.sync.dma_start(out[rows(b), :], store[b][:])

@@ -24,6 +24,7 @@ SCALE_ROWS = 4
 ENTRIES_PER_COLUMN = 16
 HALVES = 2
 H = S // HALVES
+SHARE = 128
 RUN = 4
 BY_SCALAR = (PASSES - 1, PACK - 2)
 
@@ -96,22 +97,27 @@ def tile_picked_idxput_add_e_kernel(tc, xT, mem, w1_words, w1_scales, offs, slot
         def quantise(codes, scales, woven):
             nc.vector.quantize_mx(out=codes.bitcast(FP8X4), scales=scales, in_=woven.rearrange("p c t -> p (c t)"))
 
-        for t in range(PACK - 1):
-            gather_plane(0, t)
+        gather_plane(0, 0)
+        rounded0 = keep.tile([P, T], BF16, name="rounded0")
+        nc.scalar.copy(rounded0[:], planes[0, 1][:])
+        nc.scalar.activation(picked[0][:, 1, :], rounded0[:].indirect(offs_sb[:]), COPY)
+        gather_plane(0, 2)
         gather_last_plane_and_weave(0, [woven0[:, entries(h), :] for h in range(HALVES)])
 
         for t in range(PACK - 2):
             gather_plane(1, t)
-        codes0 = keep.tile([P, S], U32, name="plane1_1", align_bytes=64)
+        codes0 = keep.tile([P, S], U32, name="codes0", align_bytes=64)
         scales0 = keep.tile([P, S], U8, name="scales0", align_bytes=64)
         quantise(codes0[:], scales0[:], woven0[:])
 
         rounded = keep.tile([P, T], BF16, name="rounded")
         for columns in column_halves:
             nc.scalar.copy(rounded[:, columns], planes[BY_SCALAR][:, columns])
-        for h in range(HALVES):
+        nc.vector.tensor_copy(picked[1][:, PACK - 2, :SHARE], planes[BY_SCALAR][:].indirect(offs_sb[:, :SHARE // ENTRIES_PER_COLUMN]))
+        for a, e in ((SHARE, H), (H, S)):
             nc.scalar.activation(
-                picked[1][:, PACK - 2, entries(h)], rounded[:].indirect(offs_sb[:, list_columns(h)]), COPY
+                picked[1][:, PACK - 2, a:e],
+                rounded[:].indirect(offs_sb[:, a // ENTRIES_PER_COLUMN:e // ENTRIES_PER_COLUMN]), COPY
             )
         gather_last_plane_and_weave(1, [woven1[h][:] for h in range(HALVES)])
 

@@ -24,9 +24,8 @@ SCALE_ROWS = 4
 ENTRIES_PER_COLUMN = 16
 HALVES = 2
 H = S // HALVES
-SHARE = 128
 RUN = 4
-BY_SCALAR = (PASSES - 1, PACK - 2)
+Q = S // 4
 
 
 def tile_picked_idxput_add_e_kernel(tc, xT, mem, w1_words, w1_scales, offs, slot, out):
@@ -35,8 +34,11 @@ def tile_picked_idxput_add_e_kernel(tc, xT, mem, w1_words, w1_scales, offs, slot
     def entries(h):
         return slice(h * H, (h + 1) * H)
 
-    def list_columns(h):
-        return slice(h * H // ENTRIES_PER_COLUMN, (h + 1) * H // ENTRIES_PER_COLUMN)
+    def quarter(q):
+        return slice(q * Q, (q + 1) * Q)
+
+    def list_columns(e):
+        return slice(e.start // ENTRIES_PER_COLUMN, e.stop // ENTRIES_PER_COLUMN)
 
     def rows(b):
         return slice(b * P, (b + 1) * P)
@@ -49,28 +51,23 @@ def tile_picked_idxput_add_e_kernel(tc, xT, mem, w1_words, w1_scales, offs, slot
         slot_sb = keep.tile([P, S // ENTRIES_PER_COLUMN], U16, name="slot_sb")
         w_codes = keep.tile([P, PASSES, N], U32, name="w_codes", align_bytes=64)
         w_scales = keep.tile([P, PASSES, N], U8, name="w_scales", align_bytes=64)
-        nc.gpsimd.memset(w_scales[:].bitcast(I32), 0)
+        nc.vector.memset(w_scales[:].bitcast(I32), 0)
 
         x_rows = xT.rearrange("(z p t) c -> z t p c", z=PASSES, t=PACK)
         w_words = w1_words.rearrange("z p n t -> p z (n t)").bitcast(I32)
         order = [(z, t) for z in range(PASSES) for t in range(PACK)]
         planes = {(z, t): keep.tile([P, T], F32, name=f"plane{z}_{t}", align_bytes=64) for z, t in order}
         store = [keep.tile([P, U], F32, name=f"store{b}") for b in range(BLOCKS)]
-        column_halves = [slice(c, c + T // 2) for c in range(0, T, T // 2)]
 
         for z, t in order:
             if (z, t) == order[-1]:
                 nc.sync.dma_start(slot_sb[:], slot)
-            if (z, t) == BY_SCALAR:
-                for columns in column_halves:
-                    nc.sync.dma_start(planes[z, t][:, columns], x_rows[z, t][:, columns])
-            else:
-                nc.sync.dma_start(planes[z, t][:], x_rows[z, t])
+            nc.sync.dma_start(planes[z, t][:], x_rows[z, t])
             if (z, t) == order[0]:
                 nc.sync.dma_start(offs_sb[:], offs)
+        nc.sync.dma_start(w_codes[:].bitcast(I32), w_words)
         for b in range(BLOCKS):
             nc.sync.dma_start(store[b][:], mem[rows(b), :])
-        nc.sync.dma_start(w_codes[:].bitcast(I32), w_words)
         for q in range(P // QUADRANT):
             nc.gpsimd.dma_start(
                 w_scales[QUADRANT * q:QUADRANT * q + SCALE_ROWS].bitcast(I32),
@@ -78,78 +75,99 @@ def tile_picked_idxput_add_e_kernel(tc, xT, mem, w1_words, w1_scales, offs, slot
             )
 
         picked = [keep.tile([P, PACK, S], BF16, name=f"picked{z}") for z in range(PASSES)]
-        woven0 = keep.tile([P, S, PACK], BF16, name="woven0", align_bytes=64)
-        woven1 = [keep.tile([P, H, PACK], BF16, name=f"woven1_{h}", align_bytes=64) for h in range(HALVES)]
+        woven = [keep.tile([P, S, PACK], BF16, name=f"woven{z}", align_bytes=64) for z in range(PASSES)]
+        codes = [keep.tile([P, S], U32, name=f"codes{z}", align_bytes=64) for z in range(PASSES)]
+        scales = [keep.tile([P, S], U8, name=f"scales{z}", align_bytes=64) for z in range(PASSES)]
+        whole = slice(0, S)
 
-        def gather_plane(z, t):
-            nc.vector.tensor_copy(picked[z][:, t, :], planes[z, t][:].indirect(offs_sb[:]))
+        def gather(engine, dst, window, offsets):
+            if engine == "scalar":
+                nc.scalar.activation(dst, window.indirect(offsets), COPY)
+            else:
+                nc.vector.tensor_copy(dst, window.indirect(offsets))
 
-        def gather_last_plane_and_weave(z, woven_halves):
-            for h in range(HALVES):
-                nc.vector.tensor_copy(
-                    picked[z][:, PACK - 1, entries(h)], planes[z, PACK - 1][:].indirect(offs_sb[:, list_columns(h)])
-                )
-                nc.scalar.copy(
-                    woven_halves[h].rearrange("p (c i) t -> p c t i", i=RUN),
-                    picked[z][:, :, entries(h)].rearrange("p t (c i) -> p c t i", i=RUN),
-                )
+        def pick(engine, z, t, e):
+            gather(engine, picked[z][:, t, e], planes[z, t][:], offs_sb[:, list_columns(e)])
 
-        def quantise(codes, scales, woven):
-            nc.vector.quantize_mx(out=codes.bitcast(FP8X4), scales=scales, in_=woven.rearrange("p c t -> p (c t)"))
+        def weave(engine, z, e):
+            dst = woven[z][:, e, :].rearrange("p (c i) t -> p c t i", i=RUN)
+            src = picked[z][:, :, e].rearrange("p t (c i) -> p c t i", i=RUN)
+            if engine == "scalar":
+                nc.scalar.copy(dst, src)
+            else:
+                nc.vector.tensor_copy(dst, src)
 
-        gather_plane(0, 0)
-        rounded0 = keep.tile([P, T], BF16, name="rounded0")
-        nc.scalar.copy(rounded0[:], planes[0, 1][:])
-        nc.scalar.activation(picked[0][:, 1, :], rounded0[:].indirect(offs_sb[:]), COPY)
-        gather_plane(0, 2)
-        gather_last_plane_and_weave(0, [woven0[:, entries(h), :] for h in range(HALVES)])
-
-        for t in range(PACK - 2):
-            gather_plane(1, t)
-        codes0 = keep.tile([P, S], U32, name="codes0", align_bytes=64)
-        scales0 = keep.tile([P, S], U8, name="scales0", align_bytes=64)
-        quantise(codes0[:], scales0[:], woven0[:])
-
-        rounded = keep.tile([P, T], BF16, name="rounded")
-        for columns in column_halves:
-            nc.scalar.copy(rounded[:, columns], planes[BY_SCALAR][:, columns])
-        nc.vector.tensor_copy(picked[1][:, PACK - 2, :SHARE], planes[BY_SCALAR][:].indirect(offs_sb[:, :SHARE // ENTRIES_PER_COLUMN]))
-        for a, e in ((SHARE, H), (H, S)):
-            nc.scalar.activation(
-                picked[1][:, PACK - 2, a:e],
-                rounded[:].indirect(offs_sb[:, a // ENTRIES_PER_COLUMN:e // ENTRIES_PER_COLUMN]), COPY
+        def quantise(z, e):
+            nc.vector.quantize_mx(
+                out=codes[z][:, e].bitcast(FP8X4), scales=scales[z][:, e],
+                in_=woven[z][:, e, :].rearrange("p c t -> p (c t)"),
             )
-        gather_last_plane_and_weave(1, [woven1[h][:] for h in range(HALVES)])
 
-        acc = [[psum.tile([P, H], F32, name=f"acc{h}_{b}") for b in range(BLOCKS)] for h in range(HALVES)]
+        acc = [psum.tile([P, S], F32, name=f"acc{b}") for b in range(BLOCKS)]
 
-        def multiply(h, b, z, codes, scales):
+        def multiply(h, b, z):
             nc.tensor.matmul_mx(
-                out=acc[h][b][:],
+                out=acc[b][:, entries(h)],
                 lhsT=w_codes[:, z, rows(b)].bitcast(FP8X4),
                 lhsT_scale=w_scales[:, z, rows(b)],
-                rhs=codes.bitcast(FP8X4),
-                rhs_scale=scales,
-                start=(z == 0),
-                stop=(z == PASSES - 1),
+                rhs=codes[z][:, entries(h)].bitcast(FP8X4),
+                rhs_scale=scales[z][:, entries(h)],
+                start=(z == 0 and h == 0),
+                stop=(z == PASSES - 1 and h == HALVES - 1),
             )
 
         old = [keep.tile([P, S], F32, name=f"old{b}") for b in range(BLOCKS)]
-        y = [[keep.tile([P, H], F32, name=f"y{h}_{b}") for b in range(BLOCKS)] for h in range(HALVES)]
-        for h in range(HALVES):
-            nc.vector.tensor_copy(old[h][:], store[h][:].indirect(slot_sb[:]))
-            codes1 = keep.tile([P, H], U32, name=f"codes1_{h}", align_bytes=64)
-            scales1 = keep.tile([P, H], U8, name=f"scales1_{h}", align_bytes=64)
-            quantise(codes1[:], scales1[:], woven1[h][:])
-            for b in range(BLOCKS):
-                multiply(h, b, 0, codes0[:, entries(h)], scales0[:, entries(h)])
-                multiply(h, b, 1, codes1[:], scales1[:])
-                nc.scalar.copy(y[h][b][:], acc[h][b][:])
+        fresh = [keep.tile([P, S], F32, name=f"fresh{b}") for b in range(BLOCKS)]
 
-        for h in range(HALVES):
-            for b in range(BLOCKS):
-                nc.vector.tensor_tensor(
-                    store[b][:].indirect(slot_sb[:, list_columns(h)]), y[h][b][:], old[b][:, entries(h)], ADD
-                )
+        def look_up(engine, b, e):
+            gather(engine, old[b][:, e], store[b][:], slot_sb[:, list_columns(e)])
+
+        def add_old(h):
+            nc.vector.tensor_tensor(fresh[0][:, entries(h)], acc[0][:, entries(h)], old[0][:, entries(h)], ADD)
+
+        def empty(e):
+            nc.scalar.copy(fresh[1][:, e], acc[1][:, e])
+
+        def scatter_copy(e):
+            nc.scalar.activation(store[0][:].indirect(slot_sb[:, list_columns(e)]), fresh[0][:, e], COPY)
+
+        def scatter_add(e):
+            nc.vector.tensor_tensor(store[1][:].indirect(slot_sb[:, list_columns(e)]), fresh[1][:, e], old[1][:, e], ADD)
+
+        rounded = keep.tile([P, T], BF16, name="rounded")
+        nc.scalar.copy(rounded[:], planes[0, 0][:])
+        gather("scalar", picked[0][:, 0, :], rounded[:], offs_sb[:])
+        pick("vector", 0, 1, whole)
+        pick("scalar", 0, 2, whole)
+        pick("vector", 0, 3, entries(0))
+        pick("scalar", 0, 3, entries(1))
+        weave("vector", 0, entries(0))
+        weave("scalar", 0, entries(1))
+        pick("vector", 1, 0, whole)
+        quantise(0, whole)
+        pick("scalar", 1, 1, whole)
+        pick("vector", 1, 2, entries(0))
+        pick("scalar", 1, 2, entries(1))
+        for q in range(4):
+            pick("vector" if q < 2 else "scalar", 1, 3, quarter(q))
+        for q in range(4):
+            weave("vector" if q < 2 else "scalar", 1, quarter(q))
+        quantise(1, quarter(0))
+        quantise(1, quarter(1))
+        quantise(1, entries(1))
+        for z in range(PASSES):
+            for h in range(HALVES):
+                for b in (1, 0):
+                    multiply(h, b, z)
+        look_up("scalar", 0, entries(1))
+        look_up("vector", 0, entries(0))
+        empty(whole)
+        add_old(1)
+        look_up("vector", 1, whole)
+        add_old(0)
+        scatter_copy(entries(1))
+        scatter_copy(entries(0))
+        scatter_add(whole)
+
         for b in range(BLOCKS):
             nc.sync.dma_start(out[rows(b), :], store[b][:])

@@ -49,9 +49,9 @@ def tile_picked_idxput_add_e_kernel(tc, xT, mem, w1_words, w1_scales, offs, slot
 
         offs_sb = keep.tile([P, S // ENTRIES_PER_COLUMN], U16, name="offs_sb")
         slot_sb = keep.tile([P, S // ENTRIES_PER_COLUMN], U16, name="slot_sb")
-        w_codes = keep.tile([P, PASSES, N], U32, name="w_codes", align_bytes=64)
+        w_codes = [keep.tile([P, N], U32, name=f"w_codes{z}", align_bytes=64) for z in range(PASSES)]
         w_scales = keep.tile([P, PASSES, N], U8, name="w_scales", align_bytes=64)
-        nc.vector.memset(w_scales[:].bitcast(I32), 0)
+        nc.gpsimd.memset(w_scales[:].bitcast(I32), 0)
 
         x_rows = xT.rearrange("(z p t) c -> z t p c", z=PASSES, t=PACK)
         w_words = w1_words.rearrange("z p n t -> p z (n t)").bitcast(I32)
@@ -62,17 +62,19 @@ def tile_picked_idxput_add_e_kernel(tc, xT, mem, w1_words, w1_scales, offs, slot
         for z, t in order:
             if (z, t) == order[-1]:
                 nc.sync.dma_start(slot_sb[:], slot)
+                nc.sync.dma_start(w_codes[0][:].bitcast(I32), w_words[:, 0, :])
             nc.sync.dma_start(planes[z, t][:], x_rows[z, t])
             if (z, t) == order[0]:
                 nc.sync.dma_start(offs_sb[:], offs)
-        nc.sync.dma_start(w_codes[:].bitcast(I32), w_words)
+            if (z, t) == order[1]:
+                for q in range(P // QUADRANT):
+                    nc.sync.dma_start(
+                        w_scales[QUADRANT * q:QUADRANT * q + SCALE_ROWS].bitcast(I32),
+                        w1_scales[:, SCALE_ROWS * q:SCALE_ROWS * (q + 1), :].rearrange("z r n -> r z n").bitcast(I32),
+                    )
+        nc.sync.dma_start(w_codes[1][:].bitcast(I32), w_words[:, 1, :])
         for b in range(BLOCKS):
             nc.sync.dma_start(store[b][:], mem[rows(b), :])
-        for q in range(P // QUADRANT):
-            nc.gpsimd.dma_start(
-                w_scales[QUADRANT * q:QUADRANT * q + SCALE_ROWS].bitcast(I32),
-                w1_scales[:, SCALE_ROWS * q:SCALE_ROWS * (q + 1), :].rearrange("z r n -> r z n").bitcast(I32),
-            )
 
         picked = [keep.tile([P, PACK, S], BF16, name=f"picked{z}") for z in range(PASSES)]
         woven = [keep.tile([P, S, PACK], BF16, name=f"woven{z}", align_bytes=64) for z in range(PASSES)]
@@ -103,71 +105,86 @@ def tile_picked_idxput_add_e_kernel(tc, xT, mem, w1_words, w1_scales, offs, slot
                 in_=woven[z][:, e, :].rearrange("p c t -> p (c t)"),
             )
 
-        acc = [psum.tile([P, S], F32, name=f"acc{b}") for b in range(BLOCKS)]
+        first, rest = slice(0, Q), slice(Q, S)
+        acc_first = psum.tile([P, Q], F32, name="acc_first")
+        acc_rest = psum.tile([P, S - Q], F32, name="acc_rest")
+        acc_other = psum.tile([P, S], F32, name="acc_other")
 
-        def multiply(h, b, z):
+        def multiply(acc, acc_entries, b, z, e):
             nc.tensor.matmul_mx(
-                out=acc[b][:, entries(h)],
-                lhsT=w_codes[:, z, rows(b)].bitcast(FP8X4),
+                out=acc[:, e.start - acc_entries.start:e.stop - acc_entries.start],
+                lhsT=w_codes[z][:, rows(b)].bitcast(FP8X4),
                 lhsT_scale=w_scales[:, z, rows(b)],
-                rhs=codes[z][:, entries(h)].bitcast(FP8X4),
-                rhs_scale=scales[z][:, entries(h)],
-                start=(z == 0 and h == 0),
-                stop=(z == PASSES - 1 and h == HALVES - 1),
+                rhs=codes[z][:, e].bitcast(FP8X4),
+                rhs_scale=scales[z][:, e],
+                start=(z == 0 and e.start == acc_entries.start),
+                stop=(z == PASSES - 1 and e.stop == acc_entries.stop),
             )
 
-        old = [keep.tile([P, S], F32, name=f"old{b}") for b in range(BLOCKS)]
-        fresh = [keep.tile([P, S], F32, name=f"fresh{b}") for b in range(BLOCKS)]
+        shared = keep.tile([P, 2 * S - Q], F32, name="shared")
+        old_rest, old_first, product = shared[:, :S - Q], shared[:, S - Q:S], shared[:, S - Q:]
+        old_other = keep.tile([P, S], F32, name="old_other")
+        fresh = keep.tile([P, S], F32, name="fresh")
 
-        def look_up(engine, b, e):
-            gather(engine, old[b][:, e], store[b][:], slot_sb[:, list_columns(e)])
-
-        def add_old(h):
-            nc.vector.tensor_tensor(fresh[0][:, entries(h)], acc[0][:, entries(h)], old[0][:, entries(h)], ADD)
-
-        def empty(e):
-            nc.scalar.copy(fresh[1][:, e], acc[1][:, e])
+        def look_up(engine, dst, b, e):
+            gather(engine, dst, store[b][:], slot_sb[:, list_columns(e)])
 
         def scatter_copy(e):
-            nc.scalar.activation(store[0][:].indirect(slot_sb[:, list_columns(e)]), fresh[0][:, e], COPY)
+            nc.scalar.activation(store[0][:].indirect(slot_sb[:, list_columns(e)]), fresh[:, e], COPY)
 
-        def scatter_add(e):
-            nc.vector.tensor_tensor(store[1][:].indirect(slot_sb[:, list_columns(e)]), fresh[1][:, e], old[1][:, e], ADD)
+        def weave_three(e):
+            nc.vector.tensor_copy(
+                woven[1][:, e, :PACK - 1].rearrange("p (c i) t -> p c t i", i=RUN),
+                picked[1][:, :PACK - 1, e].rearrange("p t (c i) -> p c t i", i=RUN),
+            )
+
+        def pick_last(e):
+            nc.vector.tensor_copy(woven[1][:, e, PACK - 1], planes[1, PACK - 1][:].indirect(offs_sb[:, list_columns(e)]))
 
         rounded = keep.tile([P, T], BF16, name="rounded")
         nc.scalar.copy(rounded[:], planes[0, 0][:])
         gather("scalar", picked[0][:, 0, :], rounded[:], offs_sb[:])
         pick("vector", 0, 1, whole)
-        pick("scalar", 0, 2, whole)
-        pick("vector", 0, 3, entries(0))
-        pick("scalar", 0, 3, entries(1))
-        weave("vector", 0, entries(0))
-        weave("scalar", 0, entries(1))
-        pick("vector", 1, 0, whole)
-        quantise(0, whole)
-        pick("scalar", 1, 1, whole)
-        pick("vector", 1, 2, entries(0))
+        for t in (2, 3):
+            pick("vector", 0, t, entries(0))
+            pick("scalar", 0, t, entries(1))
+        for h in range(HALVES):
+            weave("vector", 0, entries(h))
+        for h in range(HALVES):
+            quantise(0, entries(h))
+        pick("scalar", 1, 0, whole)
+        pick("vector", 1, 1, quarter(0))
+        pick("scalar", 1, 1, slice(Q, S))
+        pick("vector", 1, 2, quarter(0))
+        pick("vector", 1, 2, quarter(1))
         pick("scalar", 1, 2, entries(1))
-        for q in range(4):
-            pick("vector" if q < 2 else "scalar", 1, 3, quarter(q))
-        for q in range(4):
-            weave("vector" if q < 2 else "scalar", 1, quarter(q))
+        weave_three(quarter(0))
+        weave_three(slice(Q, 3 * Q))
+        multiply(acc_first, first, 0, 0, first)
+        multiply(acc_rest, rest, 0, 0, quarter(1))
+        multiply(acc_rest, rest, 0, 0, entries(1))
+        multiply(acc_other, whole, 1, 0, whole)
+        pick("scalar", 1, 3, quarter(3))
+        weave("scalar", 1, quarter(3))
+        pick_last(quarter(0))
+        pick_last(quarter(1))
         quantise(1, quarter(0))
-        quantise(1, quarter(1))
-        quantise(1, entries(1))
-        for z in range(PASSES):
-            for h in range(HALVES):
-                for b in (1, 0):
-                    multiply(h, b, z)
-        look_up("scalar", 0, entries(1))
-        look_up("vector", 0, entries(0))
-        empty(whole)
-        add_old(1)
-        look_up("vector", 1, whole)
-        add_old(0)
-        scatter_copy(entries(1))
-        scatter_copy(entries(0))
-        scatter_add(whole)
+        pick_last(quarter(2))
+        for q in range(1, 4):
+            quantise(1, quarter(q))
+        for q in range(4):
+            multiply(acc_first if q == 0 else acc_rest, first if q == 0 else rest, 0, 1, quarter(q))
+            multiply(acc_other, whole, 1, 1, quarter(q))
+        look_up("scalar", old_first, 0, first)
+        look_up("scalar", old_rest[:, :H], 0, slice(Q, Q + H))
+        look_up("vector", old_rest[:, H:], 0, quarter(3))
+        nc.vector.tensor_tensor(fresh[:, first], acc_first[:], old_first, ADD)
+        nc.vector.tensor_tensor(fresh[:, rest], acc_rest[:], old_rest, ADD)
+        look_up("vector", old_other[:], 1, whole)
+        scatter_copy(first)
+        nc.scalar.copy(product, acc_other[:])
+        scatter_copy(rest)
+        nc.vector.tensor_tensor(store[1][:].indirect(slot_sb[:]), product, old_other[:], ADD)
 
         for b in range(BLOCKS):
             nc.sync.dma_start(out[rows(b), :], store[b][:])

@@ -60,9 +60,6 @@ def tile_picked_idxput_add_e_kernel(tc, xT, mem, w1_words, w1_scales, offs, slot
         store = [keep.tile([P, U], F32, name=f"store{b}") for b in range(BLOCKS)]
 
         for z, t in order:
-            if (z, t) == order[-1]:
-                nc.sync.dma_start(slot_sb[:], slot)
-                nc.sync.dma_start(w_codes[0][:].bitcast(I32), w_words[:, 0, :])
             nc.sync.dma_start(planes[z, t][:], x_rows[z, t])
             if (z, t) == order[0]:
                 nc.sync.dma_start(offs_sb[:], offs)
@@ -72,7 +69,9 @@ def tile_picked_idxput_add_e_kernel(tc, xT, mem, w1_words, w1_scales, offs, slot
                         w_scales[QUADRANT * q:QUADRANT * q + SCALE_ROWS].bitcast(I32),
                         w1_scales[:, SCALE_ROWS * q:SCALE_ROWS * (q + 1), :].rearrange("z r n -> r z n").bitcast(I32),
                     )
-        nc.sync.dma_start(w_codes[1][:].bitcast(I32), w_words[:, 1, :])
+        for z in range(PASSES):
+            nc.sync.dma_start(w_codes[z][:].bitcast(I32), w_words[:, z, :])
+        nc.sync.dma_start(slot_sb[:], slot)
         for b in range(BLOCKS):
             nc.sync.dma_start(store[b][:], mem[rows(b), :])
 
@@ -110,7 +109,7 @@ def tile_picked_idxput_add_e_kernel(tc, xT, mem, w1_words, w1_scales, offs, slot
         acc_rest = psum.tile([P, S - Q], F32, name="acc_rest")
         acc_other = psum.tile([P, S], F32, name="acc_other")
 
-        def multiply(acc, acc_entries, b, z, e):
+        def multiply(acc, acc_entries, b, z, e, last=False):
             nc.tensor.matmul_mx(
                 out=acc[:, e.start - acc_entries.start:e.stop - acc_entries.start],
                 lhsT=w_codes[z][:, rows(b)].bitcast(FP8X4),
@@ -118,7 +117,7 @@ def tile_picked_idxput_add_e_kernel(tc, xT, mem, w1_words, w1_scales, offs, slot
                 rhs=codes[z][:, e].bitcast(FP8X4),
                 rhs_scale=scales[z][:, e],
                 start=(z == 0 and e.start == acc_entries.start),
-                stop=(z == PASSES - 1 and e.stop == acc_entries.stop),
+                stop=last,
             )
 
         shared = keep.tile([P, 2 * S - Q], F32, name="shared")
@@ -131,15 +130,6 @@ def tile_picked_idxput_add_e_kernel(tc, xT, mem, w1_words, w1_scales, offs, slot
 
         def scatter_copy(e):
             nc.scalar.activation(store[0][:].indirect(slot_sb[:, list_columns(e)]), fresh[:, e], COPY)
-
-        def weave_three(e):
-            nc.vector.tensor_copy(
-                woven[1][:, e, :PACK - 1].rearrange("p (c i) t -> p c t i", i=RUN),
-                picked[1][:, :PACK - 1, e].rearrange("p t (c i) -> p c t i", i=RUN),
-            )
-
-        def pick_last(e):
-            nc.vector.tensor_copy(woven[1][:, e, PACK - 1], planes[1, PACK - 1][:].indirect(offs_sb[:, list_columns(e)]))
 
         rounded = keep.tile([P, T], BF16, name="rounded")
         nc.scalar.copy(rounded[:], planes[0, 0][:])
@@ -155,26 +145,28 @@ def tile_picked_idxput_add_e_kernel(tc, xT, mem, w1_words, w1_scales, offs, slot
         pick("scalar", 1, 0, whole)
         pick("vector", 1, 1, quarter(0))
         pick("scalar", 1, 1, slice(Q, S))
-        pick("vector", 1, 2, quarter(0))
-        pick("vector", 1, 2, quarter(1))
+        pick("vector", 1, 2, entries(0))
         pick("scalar", 1, 2, entries(1))
-        weave_three(quarter(0))
-        weave_three(slice(Q, 3 * Q))
         multiply(acc_first, first, 0, 0, first)
         multiply(acc_rest, rest, 0, 0, quarter(1))
         multiply(acc_rest, rest, 0, 0, entries(1))
         multiply(acc_other, whole, 1, 0, whole)
-        pick("scalar", 1, 3, quarter(3))
+        pick("vector", 1, 3, quarter(1))
+        for q in (0, 3, 2):
+            pick("scalar", 1, 3, quarter(q))
+        weave("vector", 1, quarter(0))
+        weave("vector", 1, quarter(1))
         weave("scalar", 1, quarter(3))
-        pick_last(quarter(0))
-        pick_last(quarter(1))
         quantise(1, quarter(0))
-        pick_last(quarter(2))
-        for q in range(1, 4):
-            quantise(1, quarter(q))
-        for q in range(4):
-            multiply(acc_first if q == 0 else acc_rest, first if q == 0 else rest, 0, 1, quarter(q))
-            multiply(acc_other, whole, 1, 1, quarter(q))
+        quantise(1, quarter(1))
+        weave("vector", 1, quarter(2))
+        quantise(1, quarter(3))
+        quantise(1, quarter(2))
+        multiply(acc_first, first, 0, 1, first, last=True)
+        for q in (1, 3, 2):
+            multiply(acc_rest, rest, 0, 1, quarter(q), last=(q == 2))
+        for q in (0, 1, 3, 2):
+            multiply(acc_other, whole, 1, 1, quarter(q), last=(q == 2))
         look_up("scalar", old_first, 0, first)
         look_up("scalar", old_rest[:, :H], 0, slice(Q, Q + H))
         look_up("vector", old_rest[:, H:], 0, quarter(3))

@@ -18,30 +18,34 @@ COPY = mybir.ActivationFunctionType.Copy
 P = 128
 PACK = 4
 PASSES = K // (P * PACK)
-BLOCKS = N // P
+STRIPS = N // P
 QUADRANT = 32
 SCALE_ROWS = 4
 ENTRIES_PER_COLUMN = 16
+RUN = 4
 HALVES = 2
 H = S // HALVES
-RUN = 4
-Q = S // 4
+Q = H // 2
+SCALAR, VECTOR = "scalar", "vector"
 
 
 def tile_picked_idxput_add_e_kernel(tc, xT, mem, w1_words, w1_scales, offs, slot, out):
     nc = tc.nc
 
-    def entries(h):
+    def half(h):
         return slice(h * H, (h + 1) * H)
 
     def quarter(q):
         return slice(q * Q, (q + 1) * Q)
 
-    def list_columns(e):
-        return slice(e.start // ENTRIES_PER_COLUMN, e.stop // ENTRIES_PER_COLUMN)
+    def list_columns(entries):
+        return slice(entries.start // ENTRIES_PER_COLUMN, entries.stop // ENTRIES_PER_COLUMN)
 
-    def rows(b):
-        return slice(b * P, (b + 1) * P)
+    def rows(strip):
+        return slice(strip * P, (strip + 1) * P)
+
+    whole = slice(0, S)
+    first, rest = quarter(0), slice(Q, S)
 
     with ExitStack() as ctx:
         keep = ctx.enter_context(tc.tile_pool(name="keep", bufs=1))
@@ -57,7 +61,7 @@ def tile_picked_idxput_add_e_kernel(tc, xT, mem, w1_words, w1_scales, offs, slot
         w_words = w1_words.rearrange("z p n t -> p z (n t)").bitcast(I32)
         order = [(z, t) for z in range(PASSES) for t in range(PACK)]
         planes = {(z, t): keep.tile([P, T], F32, name=f"plane{z}_{t}", align_bytes=64) for z, t in order}
-        store = [keep.tile([P, U], F32, name=f"store{b}") for b in range(BLOCKS)]
+        store = [keep.tile([P, U], F32, name=f"store{strip}") for strip in range(STRIPS)]
 
         for z, t in order:
             nc.sync.dma_start(planes[z, t][:], x_rows[z, t])
@@ -69,114 +73,118 @@ def tile_picked_idxput_add_e_kernel(tc, xT, mem, w1_words, w1_scales, offs, slot
                         w_scales[QUADRANT * q:QUADRANT * q + SCALE_ROWS].bitcast(I32),
                         w1_scales[:, SCALE_ROWS * q:SCALE_ROWS * (q + 1), :].rearrange("z r n -> r z n").bitcast(I32),
                     )
-        for z in range(PASSES):
-            nc.sync.dma_start(w_codes[z][:].bitcast(I32), w_words[:, z, :])
-        nc.sync.dma_start(slot_sb[:], slot)
-        for b in range(BLOCKS):
-            nc.sync.dma_start(store[b][:], mem[rows(b), :])
+        nc.sync.dma_start(w_codes[0][:].bitcast(I32), w_words[:, 0, :])
+        for strip in range(STRIPS):
+            nc.sync.dma_start(w_codes[1][:, rows(strip)].bitcast(I32), w_words[:, 1, rows(strip)])
+            if strip == 0:
+                nc.sync.dma_start(slot_sb[:], slot)
+            nc.sync.dma_start(store[strip][:], mem[rows(strip), :])
 
         picked = [keep.tile([P, PACK, S], BF16, name=f"picked{z}") for z in range(PASSES)]
         woven = [keep.tile([P, S, PACK], BF16, name=f"woven{z}", align_bytes=64) for z in range(PASSES)]
         codes = [keep.tile([P, S], U32, name=f"codes{z}", align_bytes=64) for z in range(PASSES)]
         scales = [keep.tile([P, S], U8, name=f"scales{z}", align_bytes=64) for z in range(PASSES)]
-        whole = slice(0, S)
 
         def gather(engine, dst, window, offsets):
-            if engine == "scalar":
+            if engine == SCALAR:
                 nc.scalar.activation(dst, window.indirect(offsets), COPY)
             else:
                 nc.vector.tensor_copy(dst, window.indirect(offsets))
 
-        def pick(engine, z, t, e):
-            gather(engine, picked[z][:, t, e], planes[z, t][:], offs_sb[:, list_columns(e)])
+        def pick(engine, z, t, entries):
+            gather(engine, picked[z][:, t, entries], planes[z, t][:], offs_sb[:, list_columns(entries)])
 
-        def weave(engine, z, e):
-            dst = woven[z][:, e, :].rearrange("p (c i) t -> p c t i", i=RUN)
-            src = picked[z][:, :, e].rearrange("p t (c i) -> p c t i", i=RUN)
-            if engine == "scalar":
+        def weave(engine, z, entries):
+            dst = woven[z][:, entries, :].rearrange("p (c i) t -> p c t i", i=RUN)
+            src = picked[z][:, :, entries].rearrange("p t (c i) -> p c t i", i=RUN)
+            if engine == SCALAR:
                 nc.scalar.copy(dst, src)
             else:
                 nc.vector.tensor_copy(dst, src)
 
-        def quantise(z, e):
+        def quantise(z, entries):
             nc.vector.quantize_mx(
-                out=codes[z][:, e].bitcast(FP8X4), scales=scales[z][:, e],
-                in_=woven[z][:, e, :].rearrange("p c t -> p (c t)"),
+                out=codes[z][:, entries].bitcast(FP8X4),
+                scales=scales[z][:, entries],
+                in_=woven[z][:, entries, :].rearrange("p c t -> p (c t)"),
             )
 
-        first, rest = slice(0, Q), slice(Q, S)
         acc_first = psum.tile([P, Q], F32, name="acc_first")
         acc_rest = psum.tile([P, S - Q], F32, name="acc_rest")
-        acc_other = psum.tile([P, S], F32, name="acc_other")
+        acc_strip1 = psum.tile([P, S], F32, name="acc_strip1")
 
-        def multiply(acc, acc_entries, b, z, e, last=False):
+        def multiply(acc, acc_entries, strip, z, entries, last=False):
             nc.tensor.matmul_mx(
-                out=acc[:, e.start - acc_entries.start:e.stop - acc_entries.start],
-                lhsT=w_codes[z][:, rows(b)].bitcast(FP8X4),
-                lhsT_scale=w_scales[:, z, rows(b)],
-                rhs=codes[z][:, e].bitcast(FP8X4),
-                rhs_scale=scales[z][:, e],
-                start=(z == 0 and e.start == acc_entries.start),
+                out=acc[:, entries.start - acc_entries.start:entries.stop - acc_entries.start],
+                lhsT=w_codes[z][:, rows(strip)].bitcast(FP8X4),
+                lhsT_scale=w_scales[:, z, rows(strip)],
+                rhs=codes[z][:, entries].bitcast(FP8X4),
+                rhs_scale=scales[z][:, entries],
+                start=(z == 0 and entries.start == acc_entries.start),
                 stop=last,
             )
 
         shared = keep.tile([P, 2 * S - Q], F32, name="shared")
-        old_rest, old_first, product = shared[:, :S - Q], shared[:, S - Q:S], shared[:, S - Q:]
-        old_other = keep.tile([P, S], F32, name="old_other")
-        fresh = keep.tile([P, S], F32, name="fresh")
+        old_rest, old_first, product1 = shared[:, :S - Q], shared[:, S - Q:S], shared[:, S - Q:]
+        old1 = keep.tile([P, S], F32, name="old1")
+        new0 = keep.tile([P, S], F32, name="new0")
 
-        def look_up(engine, dst, b, e):
-            gather(engine, dst, store[b][:], slot_sb[:, list_columns(e)])
+        def look_up(engine, dst, strip, entries):
+            gather(engine, dst, store[strip][:], slot_sb[:, list_columns(entries)])
 
-        def scatter_copy(e):
-            nc.scalar.activation(store[0][:].indirect(slot_sb[:, list_columns(e)]), fresh[:, e], COPY)
+        def scatter_strip0(entries):
+            nc.scalar.activation(store[0][:].indirect(slot_sb[:, list_columns(entries)]), new0[:, entries], COPY)
 
         rounded = keep.tile([P, T], BF16, name="rounded")
         nc.scalar.copy(rounded[:], planes[0, 0][:])
-        gather("scalar", picked[0][:, 0, :], rounded[:], offs_sb[:])
-        pick("vector", 0, 1, whole)
-        for t in (2, 3):
-            pick("vector", 0, t, entries(0))
-            pick("scalar", 0, t, entries(1))
+        gather(SCALAR, picked[0][:, 0, :], rounded[:], offs_sb[:])
+        pick(VECTOR, 0, 1, whole)
+        for t in range(2, PACK):
+            pick(VECTOR, 0, t, half(0))
+            pick(SCALAR, 0, t, half(1))
         for h in range(HALVES):
-            weave("vector", 0, entries(h))
+            weave(VECTOR, 0, half(h))
         for h in range(HALVES):
-            quantise(0, entries(h))
-        pick("scalar", 1, 0, whole)
-        pick("vector", 1, 1, quarter(0))
-        pick("scalar", 1, 1, slice(Q, S))
-        pick("vector", 1, 2, entries(0))
-        pick("scalar", 1, 2, entries(1))
+            quantise(0, half(h))
+
+        pick(SCALAR, 1, 0, whole)
+        pick(VECTOR, 1, 1, first)
+        pick(SCALAR, 1, 1, rest)
+        pick(VECTOR, 1, 2, half(0))
+        pick(SCALAR, 1, 2, half(1))
         multiply(acc_first, first, 0, 0, first)
         multiply(acc_rest, rest, 0, 0, quarter(1))
-        multiply(acc_rest, rest, 0, 0, entries(1))
-        multiply(acc_other, whole, 1, 0, whole)
-        pick("vector", 1, 3, quarter(1))
+        multiply(acc_rest, rest, 0, 0, half(1))
+        multiply(acc_strip1, whole, 1, 0, whole)
+
+        pick(VECTOR, 1, 3, quarter(1))
         for q in (0, 3, 2):
-            pick("scalar", 1, 3, quarter(q))
-        weave("vector", 1, quarter(0))
-        weave("vector", 1, quarter(1))
-        weave("scalar", 1, quarter(3))
+            pick(SCALAR, 1, 3, quarter(q))
+        weave(VECTOR, 1, quarter(0))
+        weave(VECTOR, 1, quarter(1))
+        weave(SCALAR, 1, quarter(3))
         quantise(1, quarter(0))
         quantise(1, quarter(1))
-        weave("vector", 1, quarter(2))
+        weave(VECTOR, 1, quarter(2))
         quantise(1, quarter(3))
         quantise(1, quarter(2))
         multiply(acc_first, first, 0, 1, first, last=True)
-        for q in (1, 3, 2):
-            multiply(acc_rest, rest, 0, 1, quarter(q), last=(q == 2))
-        for q in (0, 1, 3, 2):
-            multiply(acc_other, whole, 1, 1, quarter(q), last=(q == 2))
-        look_up("scalar", old_first, 0, first)
-        look_up("scalar", old_rest[:, :H], 0, slice(Q, Q + H))
-        look_up("vector", old_rest[:, H:], 0, quarter(3))
-        nc.vector.tensor_tensor(fresh[:, first], acc_first[:], old_first, ADD)
-        nc.vector.tensor_tensor(fresh[:, rest], acc_rest[:], old_rest, ADD)
-        look_up("vector", old_other[:], 1, whole)
-        scatter_copy(first)
-        nc.scalar.copy(product, acc_other[:])
-        scatter_copy(rest)
-        nc.vector.tensor_tensor(store[1][:].indirect(slot_sb[:]), product, old_other[:], ADD)
+        multiply(acc_rest, rest, 0, 1, quarter(1))
+        multiply(acc_rest, rest, 0, 1, quarter(3))
+        multiply(acc_rest, rest, 0, 1, quarter(2), last=True)
+        multiply(acc_strip1, whole, 1, 1, whole, last=True)
 
-        for b in range(BLOCKS):
-            nc.sync.dma_start(out[rows(b), :], store[b][:])
+        look_up(SCALAR, old_first, 0, first)
+        look_up(SCALAR, old_rest[:, :H], 0, slice(Q, Q + H))
+        look_up(VECTOR, old_rest[:, H:], 0, quarter(3))
+        nc.vector.tensor_tensor(new0[:, first], acc_first[:], old_first, ADD)
+        nc.vector.tensor_tensor(new0[:, rest], acc_rest[:], old_rest, ADD)
+        look_up(VECTOR, old1[:], 1, whole)
+
+        scatter_strip0(first)
+        nc.scalar.copy(product1, acc_strip1[:])
+        scatter_strip0(rest)
+        nc.vector.tensor_tensor(store[1][:].indirect(slot_sb[:]), product1, old1[:], ADD)
+
+        for strip in range(STRIPS):
+            nc.sync.dma_start(out[rows(strip), :], store[strip][:])

@@ -27,6 +27,7 @@ HALVES = 2
 H = S // HALVES
 Q = H // 2
 SCALAR, VECTOR = "scalar", "vector"
+X_LOADS = [(0, 0, 2), (0, 2, 2), (1, 0, 2), (1, 2, 1), (1, 3, 1)]
 
 
 def tile_picked_idxput_add_e_kernel(tc, xT, mem, w1_words, w1_scales, offs, slot, out):
@@ -53,34 +54,32 @@ def tile_picked_idxput_add_e_kernel(tc, xT, mem, w1_words, w1_scales, offs, slot
 
         offs_sb = keep.tile([P, S // ENTRIES_PER_COLUMN], U16, name="offs_sb")
         slot_sb = keep.tile([P, S // ENTRIES_PER_COLUMN], U16, name="slot_sb")
-        w_codes = [keep.tile([P, N], U32, name=f"w_codes{z}", align_bytes=64) for z in range(PASSES)]
+        w_codes = keep.tile([P, PASSES, N], U32, name="w_codes", align_bytes=64)
         w_scales = keep.tile([P, PASSES, N], U8, name="w_scales", align_bytes=64)
         nc.gpsimd.memset(w_scales[:].bitcast(I32), 0)
 
-        x_rows = xT.rearrange("(z p t) c -> z t p c", z=PASSES, t=PACK)
-        w_words = w1_words.rearrange("z p n t -> p z (n t)").bitcast(I32)
-        order = [(z, t) for z in range(PASSES) for t in range(PACK)]
-        planes = {(z, t): keep.tile([P, T], F32, name=f"plane{z}_{t}", align_bytes=64) for z, t in order}
+        x_rows = xT.rearrange("(z p t) c -> z p t c", z=PASSES, t=PACK)
         store = [keep.tile([P, U], F32, name=f"store{strip}") for strip in range(STRIPS)]
 
-        for z, t in order:
-            nc.sync.dma_start(planes[z, t][:], x_rows[z, t])
-            if (z, t) == order[0]:
-                nc.sync.dma_start(offs_sb[:], offs)
-            if (z, t) == order[1]:
+        planes = {}
+        nc.sync.dma_start(offs_sb[:], offs)
+        for i, (z, t0, count) in enumerate(X_LOADS):
+            loaded = keep.tile([P, count, T], F32, name=f"planes{i}", align_bytes=64)
+            nc.sync.dma_start(loaded[:], x_rows[z, :, t0:t0 + count, :])
+            for t in range(count):
+                planes[z, t0 + t] = loaded[:, t, :]
+            if i == 0:
                 for q in range(P // QUADRANT):
                     nc.sync.dma_start(
                         w_scales[QUADRANT * q:QUADRANT * q + SCALE_ROWS].bitcast(I32),
                         w1_scales[:, SCALE_ROWS * q:SCALE_ROWS * (q + 1), :].rearrange("z r n -> r z n").bitcast(I32),
                     )
-        nc.sync.dma_start(w_codes[0][:].bitcast(I32), w_words[:, 0, :])
+        nc.sync.dma_start(w_codes[:].bitcast(I32), w1_words.rearrange("z p n t -> p z (n t)").bitcast(I32))
+        nc.sync.dma_start(slot_sb[:], slot)
         for strip in range(STRIPS):
-            nc.sync.dma_start(w_codes[1][:, rows(strip)].bitcast(I32), w_words[:, 1, rows(strip)])
-            if strip == 0:
-                nc.sync.dma_start(slot_sb[:], slot)
             nc.sync.dma_start(store[strip][:], mem[rows(strip), :])
 
-        picked = [keep.tile([P, PACK, S], BF16, name=f"picked{z}") for z in range(PASSES)]
+        picked = [keep.tile([P, PACK, S], F32, name=f"picked{z}") for z in range(PASSES)]
         woven = [keep.tile([P, S, PACK], BF16, name=f"woven{z}", align_bytes=64) for z in range(PASSES)]
         codes = [keep.tile([P, S], U32, name=f"codes{z}", align_bytes=64) for z in range(PASSES)]
         scales = [keep.tile([P, S], U8, name=f"scales{z}", align_bytes=64) for z in range(PASSES)]
@@ -92,7 +91,7 @@ def tile_picked_idxput_add_e_kernel(tc, xT, mem, w1_words, w1_scales, offs, slot
                 nc.vector.tensor_copy(dst, window.indirect(offsets))
 
         def pick(engine, z, t, entries):
-            gather(engine, picked[z][:, t, entries], planes[z, t][:], offs_sb[:, list_columns(entries)])
+            gather(engine, picked[z][:, t, entries], planes[z, t], offs_sb[:, list_columns(entries)])
 
         def weave(engine, z, entries):
             dst = woven[z][:, entries, :].rearrange("p (c i) t -> p c t i", i=RUN)
@@ -116,7 +115,7 @@ def tile_picked_idxput_add_e_kernel(tc, xT, mem, w1_words, w1_scales, offs, slot
         def multiply(acc, acc_entries, strip, z, entries, last=False):
             nc.tensor.matmul_mx(
                 out=acc[:, entries.start - acc_entries.start:entries.stop - acc_entries.start],
-                lhsT=w_codes[z][:, rows(strip)].bitcast(FP8X4),
+                lhsT=w_codes[:, z, rows(strip)].bitcast(FP8X4),
                 lhsT_scale=w_scales[:, z, rows(strip)],
                 rhs=codes[z][:, entries].bitcast(FP8X4),
                 rhs_scale=scales[z][:, entries],
@@ -135,21 +134,20 @@ def tile_picked_idxput_add_e_kernel(tc, xT, mem, w1_words, w1_scales, offs, slot
         def scatter_strip0(entries):
             nc.scalar.activation(store[0][:].indirect(slot_sb[:, list_columns(entries)]), new0[:, entries], COPY)
 
-        rounded = keep.tile([P, T], BF16, name="rounded")
-        nc.scalar.copy(rounded[:], planes[0, 0][:])
-        gather(SCALAR, picked[0][:, 0, :], rounded[:], offs_sb[:])
+        pick(SCALAR, 0, 0, first)
         pick(VECTOR, 0, 1, whole)
-        for t in range(2, PACK):
-            pick(VECTOR, 0, t, half(0))
-            pick(SCALAR, 0, t, half(1))
-        for h in range(HALVES):
-            weave(VECTOR, 0, half(h))
+        pick(VECTOR, 0, 0, rest)
+        pick(SCALAR, 0, 2, whole)
+        pick(VECTOR, 0, 3, whole)
+        weave(SCALAR, 0, quarter(3))
+        weave(VECTOR, 0, half(0))
+        weave(VECTOR, 0, quarter(2))
         for h in range(HALVES):
             quantise(0, half(h))
 
         pick(SCALAR, 1, 0, whole)
-        pick(VECTOR, 1, 1, first)
-        pick(SCALAR, 1, 1, rest)
+        pick(VECTOR, 1, 1, rest)
+        pick(SCALAR, 1, 1, first)
         pick(VECTOR, 1, 2, half(0))
         pick(SCALAR, 1, 2, half(1))
         multiply(acc_first, first, 0, 0, first)

@@ -27,7 +27,7 @@ HALVES = 2
 H = S // HALVES
 Q = H // 2
 SCALAR, VECTOR = "scalar", "vector"
-X_LOADS = [(0, 0, 2), (0, 2, 2), (1, 0, 2), (1, 2, 1), (1, 3, 1)]
+X_LOADS = [(0, 0, 2), (0, 2, 2), (1, 0, 1), (1, 1, 2), (1, 3, 1)]
 
 
 def tile_picked_idxput_add_e_kernel(tc, xT, mem, w1_words, w1_scales, offs, slot, out):
@@ -146,10 +146,8 @@ def tile_picked_idxput_add_e_kernel(tc, xT, mem, w1_words, w1_scales, offs, slot
             quantise(0, half(h))
 
         pick(SCALAR, 1, 0, whole)
-        pick(VECTOR, 1, 1, rest)
-        pick(SCALAR, 1, 1, first)
-        pick(VECTOR, 1, 2, half(0))
-        pick(SCALAR, 1, 2, half(1))
+        pick(VECTOR, 1, 1, whole)
+        pick(SCALAR, 1, 2, whole)
         multiply(acc_first, first, 0, 0, first)
         multiply(acc_rest, rest, 0, 0, quarter(1))
         multiply(acc_rest, rest, 0, 0, half(1))

@@ -62,18 +62,18 @@ def tile_picked_idxput_add_e_kernel(tc, xT, mem, w1_words, w1_scales, offs, slot
         store = [keep.tile([P, U], F32, name=f"store{strip}") for strip in range(STRIPS)]
 
         planes = {}
-        nc.sync.dma_start(offs_sb[:], offs)
         for i, (z, t0, count) in enumerate(X_LOADS):
             loaded = keep.tile([P, count, T], F32, name=f"planes{i}", align_bytes=64)
             nc.sync.dma_start(loaded[:], x_rows[z, :, t0:t0 + count, :])
             for t in range(count):
                 planes[z, t0 + t] = loaded[:, t, :]
             if i == 0:
-                for q in range(P // QUADRANT):
-                    nc.sync.dma_start(
-                        w_scales[QUADRANT * q:QUADRANT * q + SCALE_ROWS].bitcast(I32),
-                        w1_scales[:, SCALE_ROWS * q:SCALE_ROWS * (q + 1), :].rearrange("z r n -> r z n").bitcast(I32),
-                    )
+                nc.sync.dma_start(offs_sb[:], offs)
+        for q in range(P // QUADRANT):
+            nc.sync.dma_start(
+                w_scales[QUADRANT * q:QUADRANT * q + SCALE_ROWS].bitcast(I32),
+                w1_scales[:, SCALE_ROWS * q:SCALE_ROWS * (q + 1), :].rearrange("z r n -> r z n").bitcast(I32),
+            )
         nc.sync.dma_start(w_codes[:].bitcast(I32), w1_words.rearrange("z p n t -> p z (n t)").bitcast(I32))
         nc.sync.dma_start(slot_sb[:], slot)
         for strip in range(STRIPS):

@@ -153,15 +153,16 @@ def tile_picked_idxput_add_e_kernel(tc, xT, mem, w1_words, w1_scales, offs, slot
         multiply(acc_rest, rest, 0, 0, half(1))
         multiply(acc_strip1, whole, 1, 0, whole)
 
-        pick(VECTOR, 1, 3, quarter(1))
-        for q in (0, 3, 2):
-            pick(SCALAR, 1, 3, quarter(q))
+        pick(VECTOR, 1, 3, quarter(0))
+        pick(SCALAR, 1, 3, quarter(3))
+        pick(VECTOR, 1, 3, quarter(2))
+        pick(SCALAR, 1, 3, quarter(1))
         weave(VECTOR, 1, quarter(0))
-        weave(VECTOR, 1, quarter(1))
         weave(SCALAR, 1, quarter(3))
+        weave(VECTOR, 1, quarter(1))
         quantise(1, quarter(0))
-        quantise(1, quarter(1))
         weave(VECTOR, 1, quarter(2))
+        quantise(1, quarter(1))
         quantise(1, quarter(3))
         quantise(1, quarter(2))
         multiply(acc_first, first, 0, 1, first, last=True)

@@ -47,6 +47,7 @@ def tile_picked_idxput_add_e_kernel(tc, xT, mem, w1_words, w1_scales, offs, slot
 
     whole = slice(0, S)
     first, rest = quarter(0), slice(Q, S)
+    cut = H + Q // 2
 
     with ExitStack() as ctx:
         keep = ctx.enter_context(tc.tile_pool(name="keep", bufs=1))
@@ -172,8 +173,8 @@ def tile_picked_idxput_add_e_kernel(tc, xT, mem, w1_words, w1_scales, offs, slot
         multiply(acc_strip1, whole, 1, 1, whole, last=True)
 
         look_up(SCALAR, old_first, 0, first)
-        look_up(SCALAR, old_rest[:, :H], 0, slice(Q, Q + H))
-        look_up(VECTOR, old_rest[:, H:], 0, quarter(3))
+        look_up(SCALAR, old_rest[:, :cut - Q], 0, slice(Q, cut))
+        look_up(VECTOR, old_rest[:, cut - Q:], 0, slice(cut, S))
         nc.vector.tensor_tensor(new0[:, first], acc_first[:], old_first, ADD)
         nc.vector.tensor_tensor(new0[:, rest], acc_rest[:], old_rest, ADD)
         look_up(VECTOR, old1[:], 1, whole)

@@ -20,6 +20,7 @@ PACK = 4
 PASSES = K // (P * PACK)
 STRIPS = N // P
 QUADRANT = 32
+QUADRANTS = P // QUADRANT
 SCALE_ROWS = 4
 ENTRIES_PER_COLUMN = 16
 RUN = 4
@@ -59,6 +60,12 @@ def tile_picked_idxput_add_e_kernel(tc, xT, mem, w1_words, w1_scales, offs, slot
         w_scales = keep.tile([P, PASSES, N], U8, name="w_scales", align_bytes=64)
         nc.gpsimd.memset(w_scales[:].bitcast(I32), 0)
 
+        staged = keep.tile([SCALE_ROWS, PASSES * QUADRANTS, N], U8, name="staged", align_bytes=64)
+
+        nc.sync.dma_start(
+            staged[:].bitcast(I32), w1_scales.rearrange("z (q r) n -> r (z q) n", r=SCALE_ROWS).bitcast(I32)
+        )
+
         x_rows = xT.rearrange("(z p t) c -> z p t c", z=PASSES, t=PACK)
         store = [keep.tile([P, U], F32, name=f"store{strip}") for strip in range(STRIPS)]
 
@@ -70,15 +77,17 @@ def tile_picked_idxput_add_e_kernel(tc, xT, mem, w1_words, w1_scales, offs, slot
                 planes[z, t0 + t] = loaded[:, t, :]
             if i == 0:
                 nc.sync.dma_start(offs_sb[:], offs)
-        for q in range(P // QUADRANT):
-            nc.sync.dma_start(
-                w_scales[QUADRANT * q:QUADRANT * q + SCALE_ROWS].bitcast(I32),
-                w1_scales[:, SCALE_ROWS * q:SCALE_ROWS * (q + 1), :].rearrange("z r n -> r z n").bitcast(I32),
-            )
         nc.sync.dma_start(w_codes[:].bitcast(I32), w1_words.rearrange("z p n t -> p z (n t)").bitcast(I32))
         nc.sync.dma_start(slot_sb[:], slot)
         for strip in range(STRIPS):
             nc.sync.dma_start(store[strip][:], mem[rows(strip), :])
+
+        for q in range(QUADRANTS):
+            dst, src = w_scales[QUADRANT * q:QUADRANT * q + SCALE_ROWS], staged[:, q::QUADRANTS, :]
+            if q == 0:
+                nc.scalar.copy(dst.bitcast(U32), src.bitcast(U32))
+            else:
+                nc.vector.tensor_copy(dst.bitcast(I32), src.bitcast(I32))
 
         picked = [keep.tile([P, PACK, S], F32, name=f"picked{z}") for z in range(PASSES)]
         woven = [keep.tile([P, S, PACK], BF16, name=f"woven{z}", align_bytes=64) for z in range(PASSES)]
@@ -135,9 +144,8 @@ def tile_picked_idxput_add_e_kernel(tc, xT, mem, w1_words, w1_scales, offs, slot
         def scatter_strip0(entries):
             nc.scalar.activation(store[0][:].indirect(slot_sb[:, list_columns(entries)]), new0[:, entries], COPY)
 
-        pick(SCALAR, 0, 0, first)
+        pick(SCALAR, 0, 0, whole)
         pick(VECTOR, 0, 1, whole)
-        pick(VECTOR, 0, 0, rest)
         pick(SCALAR, 0, 2, whole)
         pick(VECTOR, 0, 3, whole)
         weave(SCALAR, 0, quarter(3))

@@ -23,12 +23,11 @@ QUADRANT = 32
 QUADRANTS = P // QUADRANT
 SCALE_ROWS = 4
 ENTRIES_PER_COLUMN = 16
-RUN = 4
+PAIR = 2
 HALVES = 2
 H = S // HALVES
 Q = H // 2
 SCALAR, VECTOR = "scalar", "vector"
-X_LOADS = [(0, 0, 2), (0, 2, 2), (1, 0, 1), (1, 1, 2), (1, 3, 1)]
 
 
 def tile_picked_idxput_add_e_kernel(tc, xT, mem, w1_words, w1_scales, offs, slot, out):
@@ -48,7 +47,7 @@ def tile_picked_idxput_add_e_kernel(tc, xT, mem, w1_words, w1_scales, offs, slot
 
     whole = slice(0, S)
     first, rest = quarter(0), slice(Q, S)
-    cut = H + Q // 2
+    cut = H + Q // 4
 
     with ExitStack() as ctx:
         keep = ctx.enter_context(tc.tile_pool(name="keep", bufs=1))
@@ -70,13 +69,12 @@ def tile_picked_idxput_add_e_kernel(tc, xT, mem, w1_words, w1_scales, offs, slot
         store = [keep.tile([P, U], F32, name=f"store{strip}") for strip in range(STRIPS)]
 
         planes = {}
-        for i, (z, t0, count) in enumerate(X_LOADS):
-            loaded = keep.tile([P, count, T], F32, name=f"planes{i}", align_bytes=64)
-            nc.sync.dma_start(loaded[:], x_rows[z, :, t0:t0 + count, :])
-            for t in range(count):
-                planes[z, t0 + t] = loaded[:, t, :]
-            if i == 0:
-                nc.sync.dma_start(offs_sb[:], offs)
+        for z in range(PASSES):
+            for t in range(PACK):
+                planes[z, t] = keep.tile([P, T], F32, name=f"plane{z}{t}", align_bytes=64)
+                nc.sync.dma_start(planes[z, t][:], x_rows[z, :, t, :])
+                if (z, t) == (0, 0):
+                    nc.sync.dma_start(offs_sb[:], offs)
         nc.sync.dma_start(w_codes[:].bitcast(I32), w1_words.rearrange("z p n t -> p z (n t)").bitcast(I32))
         nc.sync.dma_start(slot_sb[:], slot)
         for strip in range(STRIPS):
@@ -89,7 +87,11 @@ def tile_picked_idxput_add_e_kernel(tc, xT, mem, w1_words, w1_scales, offs, slot
             else:
                 nc.vector.tensor_copy(dst.bitcast(I32), src.bitcast(I32))
 
-        picked = [keep.tile([P, PACK, S], F32, name=f"picked{z}") for z in range(PASSES)]
+        paired = {
+            (z, q): keep.tile([P, PACK // PAIR, Q, PAIR], BF16, name=f"paired{z}{q}", align_bytes=64)
+            for z in range(PASSES)
+            for q in range(S // Q)
+        }
         woven = [keep.tile([P, S, PACK], BF16, name=f"woven{z}", align_bytes=64) for z in range(PASSES)]
         codes = [keep.tile([P, S], U32, name=f"codes{z}", align_bytes=64) for z in range(PASSES)]
         scales = [keep.tile([P, S], U8, name=f"scales{z}", align_bytes=64) for z in range(PASSES)]
@@ -100,16 +102,22 @@ def tile_picked_idxput_add_e_kernel(tc, xT, mem, w1_words, w1_scales, offs, slot
             else:
                 nc.vector.tensor_copy(dst, window.indirect(offsets))
 
-        def pick(engine, z, t, entries):
-            gather(engine, picked[z][:, t, entries], planes[z, t], offs_sb[:, list_columns(entries)])
+        def pick(engine, z, t, q):
+            gather(engine, paired[z, q][:, t // PAIR, :, t % PAIR], planes[z, t][:], offs_sb[:, list_columns(quarter(q))])
 
-        def weave(engine, z, entries):
-            dst = woven[z][:, entries, :].rearrange("p (c i) t -> p c t i", i=RUN)
-            src = picked[z][:, :, entries].rearrange("p t (c i) -> p c t i", i=RUN)
+        def weave(engine, z, q):
+            dst = woven[z][:, quarter(q), :].rearrange("p c t -> p (c t)")
+            src = paired[z, q][:].rearrange("p u c e -> p (u c e)")
             if engine == SCALAR:
-                nc.scalar.copy(dst, src)
+                nc.scalar.copy(
+                    dst.bitcast(U32).rearrange("p (c u) -> p c u", u=PAIR),
+                    src.bitcast(U32).rearrange("p (u c) -> p c u", u=PAIR),
+                )
             else:
-                nc.vector.tensor_copy(dst, src)
+                nc.vector.tensor_copy(
+                    dst.bitcast(I32).rearrange("p (c u) -> p c u", u=PAIR),
+                    src.bitcast(I32).rearrange("p (u c) -> p c u", u=PAIR),
+                )
 
         def quantise(z, entries):
             nc.vector.quantize_mx(
@@ -144,40 +152,32 @@ def tile_picked_idxput_add_e_kernel(tc, xT, mem, w1_words, w1_scales, offs, slot
         def scatter_strip0(entries):
             nc.scalar.activation(store[0][:].indirect(slot_sb[:, list_columns(entries)]), new0[:, entries], COPY)
 
-        pick(SCALAR, 0, 0, whole)
-        pick(VECTOR, 0, 1, whole)
-        pick(SCALAR, 0, 2, whole)
-        pick(VECTOR, 0, 3, whole)
-        weave(SCALAR, 0, quarter(3))
-        weave(VECTOR, 0, half(0))
-        weave(VECTOR, 0, quarter(2))
+        owner = [VECTOR, VECTOR, SCALAR, SCALAR]
+        for t in range(PACK):
+            for q in range(S // Q):
+                pick(owner[q], 0, t, q)
+        for q in range(S // Q):
+            weave(owner[q], 0, q)
+        for q in range(S // Q):
+            pick(owner[q], 1, 0, q)
         for h in range(HALVES):
             quantise(0, half(h))
-
-        pick(SCALAR, 1, 0, whole)
-        pick(VECTOR, 1, 1, whole)
-        pick(SCALAR, 1, 2, whole)
         multiply(acc_first, first, 0, 0, first)
         multiply(acc_rest, rest, 0, 0, quarter(1))
         multiply(acc_rest, rest, 0, 0, half(1))
-        multiply(acc_strip1, whole, 1, 0, whole)
 
-        pick(VECTOR, 1, 3, quarter(0))
-        pick(SCALAR, 1, 3, quarter(3))
-        pick(VECTOR, 1, 3, quarter(2))
-        pick(SCALAR, 1, 3, quarter(1))
-        weave(VECTOR, 1, quarter(0))
-        weave(SCALAR, 1, quarter(3))
-        weave(VECTOR, 1, quarter(1))
+        for t in range(1, PACK):
+            for q in range(S // Q):
+                pick(owner[q], 1, t, q)
+        for q in range(S // Q):
+            weave(owner[q], 1, q)
         quantise(1, quarter(0))
-        weave(VECTOR, 1, quarter(2))
         quantise(1, quarter(1))
-        quantise(1, quarter(3))
-        quantise(1, quarter(2))
+        quantise(1, half(1))
         multiply(acc_first, first, 0, 1, first, last=True)
         multiply(acc_rest, rest, 0, 1, quarter(1))
-        multiply(acc_rest, rest, 0, 1, quarter(3))
-        multiply(acc_rest, rest, 0, 1, quarter(2), last=True)
+        multiply(acc_rest, rest, 0, 1, half(1), last=True)
+        multiply(acc_strip1, whole, 1, 0, whole)
         multiply(acc_strip1, whole, 1, 1, whole, last=True)
 
         look_up(SCALAR, old_first, 0, first)

@@ -20,14 +20,15 @@ PACK = 4
 PASSES = K // (P * PACK)
 STRIPS = N // P
 QUADRANT = 32
-QUADRANTS = P // QUADRANT
 SCALE_ROWS = 4
 ENTRIES_PER_COLUMN = 16
+RUN = 4
 PAIR = 2
 HALVES = 2
 H = S // HALVES
 Q = H // 2
 SCALAR, VECTOR = "scalar", "vector"
+X_LOADS = [(0, 0, 2), (0, 2, 2), (1, 0, 2), (1, 2, 1), (1, 3, 1)]
 
 
 def tile_picked_idxput_add_e_kernel(tc, xT, mem, w1_words, w1_scales, offs, slot, out):
@@ -59,39 +60,29 @@ def tile_picked_idxput_add_e_kernel(tc, xT, mem, w1_words, w1_scales, offs, slot
         w_scales = keep.tile([P, PASSES, N], U8, name="w_scales", align_bytes=64)
         nc.gpsimd.memset(w_scales[:].bitcast(I32), 0)
 
-        staged = keep.tile([SCALE_ROWS, PASSES * QUADRANTS, N], U8, name="staged", align_bytes=64)
-
-        nc.sync.dma_start(
-            staged[:].bitcast(I32), w1_scales.rearrange("z (q r) n -> r (z q) n", r=SCALE_ROWS).bitcast(I32)
-        )
-
         x_rows = xT.rearrange("(z p t) c -> z p t c", z=PASSES, t=PACK)
         store = [keep.tile([P, U], F32, name=f"store{strip}") for strip in range(STRIPS)]
 
         planes = {}
-        for z in range(PASSES):
-            for t in range(PACK):
-                planes[z, t] = keep.tile([P, T], F32, name=f"plane{z}{t}", align_bytes=64)
-                nc.sync.dma_start(planes[z, t][:], x_rows[z, :, t, :])
-                if (z, t) == (0, 0):
-                    nc.sync.dma_start(offs_sb[:], offs)
+        for i, (z, t0, count) in enumerate(X_LOADS):
+            loaded = keep.tile([P, count * T], F32, name=f"planes{i}", align_bytes=64)
+            nc.sync.dma_start(loaded[:], x_rows[z, :, t0:t0 + count, :].rearrange("p t c -> p (t c)"))
+            for t in range(count):
+                planes[z, t0 + t] = loaded[:, t * T:(t + 1) * T]
+            if i == 0:
+                nc.sync.dma_start(offs_sb[:], offs)
+        for q in range(P // QUADRANT):
+            nc.sync.dma_start(
+                w_scales[QUADRANT * q:QUADRANT * q + SCALE_ROWS].bitcast(I32),
+                w1_scales[:, SCALE_ROWS * q:SCALE_ROWS * (q + 1), :].rearrange("z r n -> r z n").bitcast(I32),
+            )
         nc.sync.dma_start(w_codes[:].bitcast(I32), w1_words.rearrange("z p n t -> p z (n t)").bitcast(I32))
         nc.sync.dma_start(slot_sb[:], slot)
         for strip in range(STRIPS):
             nc.sync.dma_start(store[strip][:], mem[rows(strip), :])
 
-        for q in range(QUADRANTS):
-            dst, src = w_scales[QUADRANT * q:QUADRANT * q + SCALE_ROWS], staged[:, q::QUADRANTS, :]
-            if q == 0:
-                nc.scalar.copy(dst.bitcast(U32), src.bitcast(U32))
-            else:
-                nc.vector.tensor_copy(dst.bitcast(I32), src.bitcast(I32))
-
-        paired = {
-            (z, q): keep.tile([P, PACK // PAIR, Q, PAIR], BF16, name=f"paired{z}{q}", align_bytes=64)
-            for z in range(PASSES)
-            for q in range(S // Q)
-        }
+        picked = [keep.tile([P, count, S], F32, name=f"picked{z}") for z, count in enumerate((PACK, PAIR))]
+        paired = [keep.tile([P, PACK // PAIR, Q, PAIR], BF16, name=f"paired{q}", align_bytes=64) for q in range(S // Q)]
         woven = [keep.tile([P, S, PACK], BF16, name=f"woven{z}", align_bytes=64) for z in range(PASSES)]
         codes = [keep.tile([P, S], U32, name=f"codes{z}", align_bytes=64) for z in range(PASSES)]
         scales = [keep.tile([P, S], U8, name=f"scales{z}", align_bytes=64) for z in range(PASSES)]
@@ -102,12 +93,26 @@ def tile_picked_idxput_add_e_kernel(tc, xT, mem, w1_words, w1_scales, offs, slot
             else:
                 nc.vector.tensor_copy(dst, window.indirect(offsets))
 
-        def pick(engine, z, t, q):
-            gather(engine, paired[z, q][:, t // PAIR, :, t % PAIR], planes[z, t][:], offs_sb[:, list_columns(quarter(q))])
+        def pick(engine, z, t, entries):
+            gather(engine, picked[z][:, t, entries], planes[z, t], offs_sb[:, list_columns(entries)])
 
-        def weave(engine, z, q):
-            dst = woven[z][:, quarter(q), :].rearrange("p c t -> p (c t)")
-            src = paired[z, q][:].rearrange("p u c e -> p (u c e)")
+        def weave(engine, z, entries):
+            dst = woven[z][:, entries, :].rearrange("p (c i) t -> p c t i", i=RUN)
+            src = picked[z][:, :, entries].rearrange("p t (c i) -> p c t i", i=RUN)
+            if engine == SCALAR:
+                nc.scalar.copy(dst, src)
+            else:
+                nc.vector.tensor_copy(dst, src)
+
+        def pick_paired(engine, t, q):
+            gather(engine, paired[q][:, 1, :, t % PAIR], planes[1, t], offs_sb[:, list_columns(quarter(q))])
+
+        def pair_up(q):
+            nc.gpsimd.tensor_copy(paired[q][:, 0, :, :], picked[1][:, :, quarter(q)].rearrange("p e c -> p c e"))
+
+        def weave_words(engine, q):
+            dst = woven[1][:, quarter(q), :].rearrange("p c t -> p (c t)")
+            src = paired[q][:].rearrange("p u c e -> p (u c e)")
             if engine == SCALAR:
                 nc.scalar.copy(
                     dst.bitcast(U32).rearrange("p (c u) -> p c u", u=PAIR),
@@ -152,32 +157,44 @@ def tile_picked_idxput_add_e_kernel(tc, xT, mem, w1_words, w1_scales, offs, slot
         def scatter_strip0(entries):
             nc.scalar.activation(store[0][:].indirect(slot_sb[:, list_columns(entries)]), new0[:, entries], COPY)
 
-        owner = [VECTOR, VECTOR, SCALAR, SCALAR]
-        for t in range(PACK):
-            for q in range(S // Q):
-                pick(owner[q], 0, t, q)
-        for q in range(S // Q):
-            weave(owner[q], 0, q)
-        for q in range(S // Q):
-            pick(owner[q], 1, 0, q)
+        pick(SCALAR, 0, 0, first)
+        pick(VECTOR, 0, 1, whole)
+        pick(VECTOR, 0, 0, rest)
+        pick(SCALAR, 0, 2, half(0))
+        pick(VECTOR, 0, 3, half(0))
+        pick(SCALAR, 0, 2, half(1))
+        pick(VECTOR, 0, 3, quarter(2))
+        pick(SCALAR, 0, 3, quarter(3))
+        weave(VECTOR, 0, half(0))
+        weave(SCALAR, 0, quarter(2))
+        weave(VECTOR, 0, quarter(3))
         for h in range(HALVES):
             quantise(0, half(h))
-        multiply(acc_first, first, 0, 0, first)
-        multiply(acc_rest, rest, 0, 0, quarter(1))
-        multiply(acc_rest, rest, 0, 0, half(1))
 
-        for t in range(1, PACK):
-            for q in range(S // Q):
-                pick(owner[q], 1, t, q)
+        owner = [VECTOR, VECTOR, SCALAR, SCALAR]
+        pick(SCALAR, 1, 0, half(0))
+        pick(VECTOR, 1, 1, quarter(1))
+        pick(SCALAR, 1, 1, quarter(0))
+        pick(VECTOR, 1, 1, half(1))
+        pick(SCALAR, 1, 0, half(1))
         for q in range(S // Q):
-            weave(owner[q], 1, q)
+            pair_up(q)
+        for t in range(PAIR, PACK):
+            for q in range(S // Q):
+                pick_paired(owner[q], t, q)
+        for q in range(S // Q):
+            weave_words(owner[q], q)
         quantise(1, quarter(0))
         quantise(1, quarter(1))
         quantise(1, half(1))
+
+        multiply(acc_first, first, 0, 0, first)
+        multiply(acc_rest, rest, 0, 0, quarter(1))
+        multiply(acc_rest, rest, 0, 0, half(1))
+        multiply(acc_strip1, whole, 1, 0, whole)
         multiply(acc_first, first, 0, 1, first, last=True)
         multiply(acc_rest, rest, 0, 1, quarter(1))
         multiply(acc_rest, rest, 0, 1, half(1), last=True)
-        multiply(acc_strip1, whole, 1, 0, whole)
         multiply(acc_strip1, whole, 1, 1, whole, last=True)
 
         look_up(SCALAR, old_first, 0, first)

@@ -48,7 +48,7 @@ def tile_picked_idxput_add_e_kernel(tc, xT, mem, w1_words, w1_scales, offs, slot
 
     whole = slice(0, S)
     first, rest = quarter(0), slice(Q, S)
-    cut = H + Q // 4
+    cut = H - Q // 4
 
     with ExitStack() as ctx:
         keep = ctx.enter_context(tc.tile_pool(name="keep", bufs=1))
@@ -197,11 +197,12 @@ def tile_picked_idxput_add_e_kernel(tc, xT, mem, w1_words, w1_scales, offs, slot
         multiply(acc_rest, rest, 0, 1, half(1), last=True)
         multiply(acc_strip1, whole, 1, 1, whole, last=True)
 
-        look_up(SCALAR, old_first, 0, first)
-        look_up(SCALAR, old_rest[:, :cut - Q], 0, slice(Q, cut))
-        look_up(VECTOR, old_rest[:, cut - Q:], 0, slice(cut, S))
+        look_up(VECTOR, old_first, 0, first)
+        look_up(VECTOR, old_rest[:, :cut - Q], 0, slice(Q, cut))
+        look_up(SCALAR, old_rest[:, cut - Q:], 0, slice(cut, S))
         nc.vector.tensor_tensor(new0[:, first], acc_first[:], old_first, ADD)
-        nc.vector.tensor_tensor(new0[:, rest], acc_rest[:], old_rest, ADD)
+        nc.vector.tensor_tensor(new0[:, Q:cut], acc_rest[:, :cut - Q], old_rest[:, :cut - Q], ADD)
+        nc.vector.tensor_tensor(new0[:, cut:], acc_rest[:, cut - Q:], old_rest[:, cut - Q:], ADD)
         look_up(VECTOR, old1[:], 1, whole)
 
         scatter_strip0(first)

@@ -24,6 +24,7 @@ SCALE_ROWS = 4
 ENTRIES_PER_COLUMN = 16
 RUN = 4
 PAIR = 2
+DMA_ALIGN = 256
 HALVES = 2
 H = S // HALVES
 Q = H // 2
@@ -56,16 +57,16 @@ def tile_picked_idxput_add_e_kernel(tc, xT, mem, w1_words, w1_scales, offs, slot
 
         offs_sb = keep.tile([P, S // ENTRIES_PER_COLUMN], U16, name="offs_sb")
         slot_sb = keep.tile([P, S // ENTRIES_PER_COLUMN], U16, name="slot_sb")
-        w_codes = keep.tile([P, PASSES, N], U32, name="w_codes", align_bytes=64)
-        w_scales = keep.tile([P, PASSES, N], U8, name="w_scales", align_bytes=64)
+        w_codes = keep.tile([P, PASSES, N], U32, name="w_codes", align_bytes=DMA_ALIGN)
+        w_scales = keep.tile([P, PASSES, N], U8, name="w_scales", align_bytes=DMA_ALIGN)
         nc.gpsimd.memset(w_scales[:].bitcast(I32), 0)
 
         x_rows = xT.rearrange("(z p t) c -> z p t c", z=PASSES, t=PACK)
-        store = [keep.tile([P, U], F32, name=f"store{strip}") for strip in range(STRIPS)]
+        store = [keep.tile([P, U], F32, name=f"store{strip}", align_bytes=DMA_ALIGN) for strip in range(STRIPS)]
 
         planes = {}
         for i, (z, t0, count) in enumerate(X_LOADS):
-            loaded = keep.tile([P, count * T], F32, name=f"planes{i}", align_bytes=64)
+            loaded = keep.tile([P, count * T], F32, name=f"planes{i}", align_bytes=DMA_ALIGN)
             nc.sync.dma_start(loaded[:], x_rows[z, :, t0:t0 + count, :].rearrange("p t c -> p (t c)"))
             for t in range(count):
                 planes[z, t0 + t] = loaded[:, t * T:(t + 1) * T]

@@ -192,10 +192,11 @@ def tile_picked_idxput_add_e_kernel(tc, xT, mem, w1_words, w1_scales, offs, slot
         multiply(acc_first, first, 0, 0, first)
         multiply(acc_rest, rest, 0, 0, quarter(1))
         multiply(acc_rest, rest, 0, 0, half(1))
-        multiply(acc_strip1, whole, 1, 0, whole)
         multiply(acc_first, first, 0, 1, first, last=True)
         multiply(acc_rest, rest, 0, 1, quarter(1))
+        multiply(acc_strip1, whole, 1, 0, half(0))
         multiply(acc_rest, rest, 0, 1, half(1), last=True)
+        multiply(acc_strip1, whole, 1, 0, half(1))
         multiply(acc_strip1, whole, 1, 1, whole, last=True)
 
         look_up(VECTOR, old_first, 0, first)

from contextlib import ExitStack

import concourse.mybir as mybir

K, T, S, N, U = 1024, 1024, 512, 256, 1024
FLOPS = 2 * K * S * N

F32 = mybir.dt.float32
BF16 = mybir.dt.bfloat16
I32 = mybir.dt.int32
U32 = mybir.dt.uint32
U16 = mybir.dt.uint16
U8 = mybir.dt.uint8
FP8X4 = mybir.dt.float8_e4m3fn_x4
ADD = mybir.AluOpType.add
COPY = mybir.ActivationFunctionType.Copy

P = 128
PACK = 4
PASSES = K // (P * PACK)
STRIPS = N // P
QUADRANT = 32
SCALE_ROWS = 4
ENTRIES_PER_COLUMN = 16
RUN = 4
PAIR = 2
DMA_ALIGN = 256
HALVES = 2
H = S // HALVES
Q = H // 2
SCALAR, VECTOR = "scalar", "vector"
X_LOADS = [(0, 0, 2), (0, 2, 2), (1, 0, 2), (1, 2, 1), (1, 3, 1)]


def tile_picked_idxput_add_e_kernel(tc, xT, mem, w1_words, w1_scales, offs, slot, out):
    nc = tc.nc

    def half(h):
        return slice(h * H, (h + 1) * H)

    def quarter(q):
        return slice(q * Q, (q + 1) * Q)

    def list_columns(entries):
        return slice(entries.start // ENTRIES_PER_COLUMN, entries.stop // ENTRIES_PER_COLUMN)

    def rows(strip):
        return slice(strip * P, (strip + 1) * P)

    whole = slice(0, S)
    first, rest = quarter(0), slice(Q, S)
    cut = H - Q // 4

    with ExitStack() as ctx:
        keep = ctx.enter_context(tc.tile_pool(name="keep", bufs=1))
        psum = ctx.enter_context(tc.psum_pool(name="psum", bufs=1))

        offs_sb = keep.tile([P, S // ENTRIES_PER_COLUMN], U16, name="offs_sb")
        slot_sb = keep.tile([P, S // ENTRIES_PER_COLUMN], U16, name="slot_sb")
        w_codes = keep.tile([P, PASSES, N], U32, name="w_codes", align_bytes=DMA_ALIGN)
        w_scales = keep.tile([P, PASSES, N], U8, name="w_scales", align_bytes=DMA_ALIGN)
        nc.gpsimd.memset(w_scales[:].bitcast(I32), 0)

        x_rows = xT.rearrange("(z p t) c -> z p t c", z=PASSES, t=PACK)
        store = [keep.tile([P, U], F32, name=f"store{strip}", align_bytes=DMA_ALIGN) for strip in range(STRIPS)]

        planes = {}
        for i, (z, t0, count) in enumerate(X_LOADS):
            loaded = keep.tile([P, count * T], F32, name=f"planes{i}", align_bytes=DMA_ALIGN)
            nc.sync.dma_start(loaded[:], x_rows[z, :, t0:t0 + count, :].rearrange("p t c -> p (t c)"))
            for t in range(count):
                planes[z, t0 + t] = loaded[:, t * T:(t + 1) * T]
            if i == 0:
                nc.sync.dma_start(offs_sb[:], offs)
        for q in range(P // QUADRANT):
            nc.sync.dma_start(
                w_scales[QUADRANT * q:QUADRANT * q + SCALE_ROWS].bitcast(I32),
                w1_scales[:, SCALE_ROWS * q:SCALE_ROWS * (q + 1), :].rearrange("z r n -> r z n").bitcast(I32),
            )
        nc.sync.dma_start(w_codes[:].bitcast(I32), w1_words.rearrange("z p n t -> p z (n t)").bitcast(I32))
        nc.sync.dma_start(slot_sb[:], slot)
        for strip in range(STRIPS):
            nc.sync.dma_start(store[strip][:], mem[rows(strip), :])

        picked = [keep.tile([P, count, S], F32, name=f"picked{z}") for z, count in enumerate((PACK, PAIR))]
        paired = [keep.tile([P, PACK // PAIR, Q, PAIR], BF16, name=f"paired{q}", align_bytes=64) for q in range(S // Q)]
        woven = [keep.tile([P, S, PACK], BF16, name=f"woven{z}", align_bytes=64) for z in range(PASSES)]
        codes = [keep.tile([P, S], U32, name=f"codes{z}", align_bytes=64) for z in range(PASSES)]
        scales = [keep.tile([P, S], U8, name=f"scales{z}", align_bytes=64) for z in range(PASSES)]

        def gather(engine, dst, window, offsets):
            if engine == SCALAR:
                nc.scalar.activation(dst, window.indirect(offsets), COPY)
            else:
                nc.vector.tensor_copy(dst, window.indirect(offsets))

        def pick(engine, z, t, entries):
            gather(engine, picked[z][:, t, entries], planes[z, t], offs_sb[:, list_columns(entries)])

        def weave(engine, z, entries):
            dst = woven[z][:, entries, :].rearrange("p (c i) t -> p c t i", i=RUN)
            src = picked[z][:, :, entries].rearrange("p t (c i) -> p c t i", i=RUN)
            if engine == SCALAR:
                nc.scalar.copy(dst, src)
            else:
                nc.vector.tensor_copy(dst, src)

        def pick_paired(engine, t, q):
            gather(engine, paired[q][:, 1, :, t % PAIR], planes[1, t], offs_sb[:, list_columns(quarter(q))])

        def pair_up(q):
            nc.gpsimd.tensor_copy(paired[q][:, 0, :, :], picked[1][:, :, quarter(q)].rearrange("p e c -> p c e"))

        def weave_words(engine, q):
            dst = woven[1][:, quarter(q), :].rearrange("p c t -> p (c t)")
            src = paired[q][:].rearrange("p u c e -> p (u c e)")
            if engine == SCALAR:
                nc.scalar.copy(
                    dst.bitcast(U32).rearrange("p (c u) -> p c u", u=PAIR),
                    src.bitcast(U32).rearrange("p (u c) -> p c u", u=PAIR),
                )
            else:
                nc.vector.tensor_copy(
                    dst.bitcast(I32).rearrange("p (c u) -> p c u", u=PAIR),
                    src.bitcast(I32).rearrange("p (u c) -> p c u", u=PAIR),
                )

        def quantise(z, entries):
            nc.vector.quantize_mx(
                out=codes[z][:, entries].bitcast(FP8X4),
                scales=scales[z][:, entries],
                in_=woven[z][:, entries, :].rearrange("p c t -> p (c t)"),
            )

        acc_first = psum.tile([P, Q], F32, name="acc_first")
        acc_rest = psum.tile([P, S - Q], F32, name="acc_rest")
        acc_strip1 = psum.tile([P, S], F32, name="acc_strip1")

        def multiply(acc, acc_entries, strip, z, entries, last=False):
            nc.tensor.matmul_mx(
                out=acc[:, entries.start - acc_entries.start:entries.stop - acc_entries.start],
                lhsT=w_codes[:, z, rows(strip)].bitcast(FP8X4),
                lhsT_scale=w_scales[:, z, rows(strip)],
                rhs=codes[z][:, entries].bitcast(FP8X4),
                rhs_scale=scales[z][:, entries],
                start=(z == 0 and entries.start == acc_entries.start),
                stop=last,
            )

        shared = keep.tile([P, 2 * S - Q], F32, name="shared")
        old_rest, old_first, product1 = shared[:, :S - Q], shared[:, S - Q:S], shared[:, S - Q:]
        old1 = keep.tile([P, S], F32, name="old1")
        new0 = keep.tile([P, S], F32, name="new0")

        def look_up(engine, dst, strip, entries):
            gather(engine, dst, store[strip][:], slot_sb[:, list_columns(entries)])

        def scatter_strip0(entries):
            nc.scalar.activation(store[0][:].indirect(slot_sb[:, list_columns(entries)]), new0[:, entries], COPY)

        pick(SCALAR, 0, 0, first)
        pick(VECTOR, 0, 1, whole)
        pick(VECTOR, 0, 0, rest)
        pick(SCALAR, 0, 2, half(0))
        pick(VECTOR, 0, 3, half(0))
        pick(SCALAR, 0, 2, half(1))
        pick(VECTOR, 0, 3, quarter(2))
        pick(SCALAR, 0, 3, quarter(3))
        weave(VECTOR, 0, half(0))
        weave(SCALAR, 0, quarter(2))
        weave(VECTOR, 0, quarter(3))
        for h in range(HALVES):
            quantise(0, half(h))

        owner = [VECTOR, VECTOR, SCALAR, SCALAR]
        pick(SCALAR, 1, 0, half(0))
        pick(VECTOR, 1, 1, quarter(1))
        pick(SCALAR, 1, 1, quarter(0))
        pick(VECTOR, 1, 1, half(1))
        pick(SCALAR, 1, 0, half(1))
        for q in range(S // Q):
            pair_up(q)
        for t in range(PAIR, PACK):
            for q in range(S // Q):
                pick_paired(owner[q], t, q)
        for q in range(S // Q):
            weave_words(owner[q], q)
        quantise(1, quarter(0))
        quantise(1, quarter(1))
        quantise(1, half(1))

        multiply(acc_first, first, 0, 0, first)
        multiply(acc_rest, rest, 0, 0, quarter(1))
        multiply(acc_rest, rest, 0, 0, half(1))
        multiply(acc_first, first, 0, 1, first, last=True)
        multiply(acc_rest, rest, 0, 1, quarter(1))
        multiply(acc_strip1, whole, 1, 0, half(0))
        multiply(acc_rest, rest, 0, 1, half(1), last=True)
        multiply(acc_strip1, whole, 1, 0, half(1))
        multiply(acc_strip1, whole, 1, 1, whole, last=True)

        look_up(VECTOR, old_first, 0, first)
        look_up(VECTOR, old_rest[:, :cut - Q], 0, slice(Q, cut))
        look_up(SCALAR, old_rest[:, cut - Q:], 0, slice(cut, S))
        nc.vector.tensor_tensor(new0[:, first], acc_first[:], old_first, ADD)
        nc.vector.tensor_tensor(new0[:, Q:cut], acc_rest[:, :cut - Q], old_rest[:, :cut - Q], ADD)
        nc.vector.tensor_tensor(new0[:, cut:], acc_rest[:, cut - Q:], old_rest[:, cut - Q:], ADD)
        look_up(VECTOR, old1[:], 1, whole)

        scatter_strip0(first)
        nc.scalar.copy(product1, acc_strip1[:])
        scatter_strip0(rest)
        nc.vector.tensor_tensor(store[1][:].indirect(slot_sb[:]), product1, old1[:], ADD)

        for strip in range(STRIPS):
            nc.sync.dma_start(out[rows(strip), :], store[strip][:])
